import numpy as np, ml_dtypes
CORES = [2,6,10,14,18,22,26,30]
N = 8
BF = ml_dtypes.bfloat16
W, C, H, CAP, RO = 2048, 1024, 1024, 96, 4
L = C >> 2
S16 = np.arange(16)
def owner(m):
    mb = np.zeros((8, W + 1), np.int32); mb[np.arange(8)[:, None, None], m] = np.arange(C)[None, :, None]
    return mb[:, :W]
def tight(m):
    return np.take_along_axis(m, np.argsort(m >= W, axis=-1, kind="stable"), -1)
def pick(a, j):
    return np.take_along_axis(a, j[:, :, None], 2)[:, :, 0]
def fill(n, order, s):
    s = np.minimum(s, 16 - n[order]); c = np.add.accumulate(s); left = W - np.add.reduce(n); n = n.copy()
    n[order] = n[order] + np.clip(left - (c - s), 0, s)
    return n
def sizes(rng):
    a = (W // C) * rng.choice(np.array([0.5, 1.0, 1.5]))
    n = fill(np.zeros(C, np.int64), rng.permutation(C), 1 + rng.poisson(a, C))
    return fill(n, rng.permutation(C), np.full(C, 16))
def seat(rng, n):
    m = np.full((C, 16), W, np.int64); m[S16 < n[:, None]] = rng.permutation(W)
    return m
def seats(rng):
    return np.stack([np.stack([seat(rng, sizes(rng)) for g in range(8)]) for q in range(N)])
def people(rng, m):
    typ = rng.integers(0, 16, (8, 24, 16)); own = np.take_along_axis(rng.integers(0, 24, (8, C)), owner(m), 1)
    ty = np.where(rng.random((8, W)) < rng.choice(np.array([0.3, 0.7, 0.95]), (8, 1)), own, rng.integers(0, 24, (8, W)))
    v = typ[np.arange(8)[:, None], ty]
    return np.clip(v + rng.integers(-3, 4, (8, W, 16)), 0, 15)
def wrap(x, a, m, li, w):
    def turn(v): return np.ascontiguousarray(v.transpose(0, 1, 3, 2)).reshape(N, 128, -1)
    return {"x0": turn(x).astype(np.float32).astype(BF), "ac": turn(a).astype(np.int32), "ml": turn(m).astype(np.int32),
            "lims": np.repeat(li, 16, axis=1).astype(np.int32), "wt": w.reshape(N, 128, 1).astype(np.int32)}
def setup_inputs(rng):
    m = seats(rng); x = np.stack([people(rng, b) for b in m])
    li = np.stack([rng.integers(30, 130, (N, 8)), rng.integers(20, 110, (N, 8))], axis=2)
    return wrap(x, rng.integers(0, W, (N, 8, H, 16)), m, li, rng.integers(0, 256, (N, 8, 16)))
def setup_inputs_ends(rng):
    ms, xs, as_, ls = [], [], [], []
    for q in range(N):
        m = []
        for g in range(8):
            n = np.zeros(C, np.int64); n[:4] = 16; n[C - 4:] = 16; o = 4 + rng.permutation(C - 8)
            n = fill(n, o, rng.choice(np.array([1, 1, 1, 16, 16, 8]), C - 8)); n = fill(n, o, np.full(C - 8, 16)); b = seat(rng, n)
            c = C - 4 + (g + q) % 4
            for v, k in ((0, 0), (W - 1, 15)):
                at = np.argwhere(b == v)[0]; b[at[0], at[1]] = b[c, k]; b[c, k] = v
            m.append(b)
        m = np.stack(m); ty = rng.integers(0, 5, (8, C, 1, 1)); ty[:, :4] = 4; ty[:, C - 4:] = 4
        edge = ((S16 != 2) & (S16 != 15))[None, None, :, None]
        val = np.where(ty == 0, True, np.where(ty == 1, False, np.where(ty == 2, rng.random((8, C, 16, 1)) < 0.5, np.where(ty == 3, rng.random((8, C, 16, 16)) < 0.5, edge))))
        x = np.zeros((8, W + 1, 16), np.int64); x[np.arange(8)[:, None, None], m] = 15 * val
        far = rng.random((8, H, 16)) < np.where(rng.random((8, H, 1)) < 0.4, 1.1, 0.55)
        ms.append(m); xs.append(x[:, :W]); as_.append(np.where(far, (W - 1) * rng.integers(0, 2, (8, H, 16)), rng.integers(0, W, (8, H, 16))))
        ls.append(np.array([[0, 0], [0, 240], [240, 0], [240, 240]])[(np.arange(8) // 2 + q) % 4])
    w = 255 * rng.integers(0, 2, (N, 8, 16)); w[:, 3::4] = 255; w[:, 1] = 0
    return wrap(np.stack(xs), np.stack(as_), np.stack(ms), np.stack(ls), w)
def setup_inputs_corners(rng):
    ms, xs, as_, ls = [], [], [], []
    for q in range(N):
        m = []; l = []; x = rng.integers(0, 16, (8, W, 16))
        for g in range(8):
            k = (g + q) & 7; n = np.zeros(C, np.int64); o = rng.permutation(C); z = 4 * rng.permutation(L); u = o[(o & 3) != 0]
            if k < 2:
                n[z[:CAP + k]] = 16; n = fill(n, u, rng.choice(np.array([1, 4, 8, 16]), len(u))); n = fill(n, u, np.full(len(u), 16))
            elif k == 2: n[:] = W // C
            elif k == 3:
                n[:] = W // C; n[o[:3]] = 0; n[o[3:6]] = 2 * (W // C)
            elif k == 4:
                n[z[:L // 2]] = 8; n = fill(n, u, rng.choice(np.array([8, 9]), len(u)))
            elif k == 5: n = fill(n, o, np.full(C, 16))
            elif k == 6:
                n[z] = 1; n = fill(n, u, rng.choice(np.array([15, 16]), len(u)))
            else:
                n = sizes(rng); x[g] = rng.integers(0, 2, (W, 16))
            m.append(seat(rng, n)); l.append(((0, 240), (0, 240), (240, 0), (0, 0), (240, 240), (240, 0), (240, 0), (int(rng.integers(2, 14)), int(rng.integers(2, 9))))[k])
        m = np.stack(m); mb = owner(m); mode = rng.integers(0, 6, (8, H, 1)); a = rng.integers(0, W, (8, H, 16)); zero = []
        for g in range(8):
            c0 = np.nonzero((mb[g] & 3) == 0)[0]
            if len(c0) == 0: c0 = np.arange(W)
            zero.append(c0[rng.integers(0, len(c0), (H, 16))])
        a = np.where(mode == 1, a[:, :, :1], np.where(mode == 2, (W - 1) * rng.integers(0, 2, (8, H, 16)), np.where(mode == 3, np.arange(H)[None, :, None] + H * rng.integers(0, W // H, (8, H, 16)),
            np.where(mode == 4, np.stack(zero), np.where(mode == 5, a[:, :, S16 & 1], a)))))
        ms.append(m); xs.append(x); as_.append(a); ls.append(np.array(l))
    w = np.where(rng.random((N, 8, 16)) < 0.5, rng.integers(0, 256, (N, 8, 16)), rng.choice(np.array([0, 1, 255]), (N, 8, 16)))
    return wrap(np.stack(xs), np.stack(as_), np.stack(ms), np.stack(ls), w)
def setup_inputs_brim(rng):
    ms, xs, as_, ls = [], [], [], []
    for q in range(N):
        m = []; l = []; x = rng.integers(0, 16, (8, W, 16)); a = rng.integers(0, W, (8, H, 16))
        for g in range(8):
            k = (g + q) & 3; n = np.zeros(C, np.int64); o = rng.permutation(C); z = 4 * rng.permutation(L); u = o[(o & 3) != 0][:L]
            if k == 1:
                n[z] = 1; n[u] = 2; n = fill(n, o, rng.choice(np.array([0, 2, 4, 6]), C)); n = fill(n, o, 8 - n[o])
            else:
                n[z] = 4; n = fill(n, rng.permutation(np.concatenate([z, u])), rng.choice(np.array([0, 1, 4, 8, 12]), 2 * L)); n = fill(n, rng.permutation(z), np.full(L, 12))
            b = seat(rng, n)
            if k == 1:
                old = b[z, rng.integers(0, n[z])]; h = rng.permutation(H)[:L]; new = h + H * rng.integers(0, W // H, L); p = np.full(W + 1, W)
                p[old] = new; p[np.setdiff1d(np.arange(W), old)] = rng.permutation(np.setdiff1d(np.arange(W), new)); b = p[b]
                x[g] = rng.integers(1, 16, (W, 16)); x[g, new] = 0
                x[g, b[u, 0]] = np.where(S16 == rng.integers(0, 16, (L, 1)), 0, 12); x[g, b[u, 1]] = np.where(S16 == rng.integers(0, 16, (L, 1)), 1, 12)
                a[g, h] = np.where((rng.random((L, 16)) < 0.25) & (S16 > 1), new[rng.integers(0, L, (L, 16))], np.where((S16 & 1) == 1, b[u, 0][:, None], b[np.roll(u, -1), 1][:, None]))
            elif k == 2:
                p = np.argsort(rng.random((L, 16)), axis=1); j = np.argsort(rng.random((L, 4)), axis=1); x[g] = rng.integers(1, 10, (W, 16))
                x[g, b[z, j[:, 0]]] = 0; x[g, b[z, j[:, 1]]] = np.where(p < 10, 15, np.where(p == 10, 1, 0)); x[g, b[z, j[:, 2]]] = np.where(p >= 6, 15, np.where(p < 2, 1, 0))
            elif k == 3:
                ty = rng.integers(0, 3, (W, 1)); x[g] = np.where(ty == 0, 15, np.where((ty == 1) & (S16 == rng.integers(0, 16, (W, 1))), 1, 0))
            m.append(b); l.append(((0, 0), (240, 0), (0, 0), (0, 239 + (g >> 2)))[k])
        ms.append(np.stack(m)); xs.append(x); as_.append(a); ls.append(np.array(l))
    return wrap(np.stack(xs), np.stack(as_), np.stack(ms), np.stack(ls), rng.integers(0, 256, (N, 8, 16)))
def setup_inputs_ties(rng):
    m = seats(rng); two = np.array([[0, 1], [7, 8], [0, 15], [3, 6]])[(np.arange(8)[None, :] + np.arange(N)[:, None]) & 3]
    pool = rng.integers(0, 2, (N, 8, 12, 16)); pool = np.where(pool == 1, two[:, :, None, 1:], two[:, :, None, :1])
    kind = rng.integers(0, 12, (N, 8, W)); x = pool[np.arange(N)[:, None, None], np.arange(8)[None, :, None], kind]
    step = two[:, :, 1] - two[:, :, 0]; li = np.stack([step * rng.integers(5, 14, (N, 8)), step * rng.integers(3, 11, (N, 8))], axis=2)
    known = rng.integers(0, W, (N, 8, 40)); k = rng.integers(0, 40, (N, 8, H * 16))
    a = np.where(rng.random((N, 8, H, 1)) < 0.5, np.take_along_axis(known, k, 2).reshape(N, 8, H, 16), rng.integers(0, W, (N, 8, H, 16)))
    return wrap(x, a, m, np.minimum(li, 240), rng.integers(0, 256, (N, 8, 16)))
def setup_inputs_spread(rng):
    x = rng.integers(0, 2 ** rng.integers(0, 5, (N, 8, W, 1)), (N, 8, W, 16)); m = []
    for q in range(N):
        for g in range(8):
            n = fill(np.zeros(C, np.int64), rng.permutation(C), rng.choice(np.array([0, 1, 1, 2, 3, 5, 16]), C)); m.append(seat(rng, fill(n, rng.permutation(C), np.full(C, 16))))
    a = np.minimum((W * rng.random((N, 8, H, 16)) ** 3).astype(np.int64), W - 1); w = np.minimum((np.exp2(8 * rng.random((N, 8, 16))) - 1).astype(np.int64), 255)
    return wrap(x, a, np.stack(m).reshape(N, 8, C, 16), rng.integers(0, 241, (N, 8, 2)), w)
def check_inputs(d):
    bad = []
    for k, lo, hi in (("x0", 0, 15), ("ac", 0, W - 1), ("ml", 0, W), ("lims", 0, 240), ("wt", 0, 255)):
        a = np.asarray(d[k]).astype(np.float64)
        if not (np.min(a) >= lo and np.max(a) <= hi): bad.append("range of " + k)
    a = np.asarray(d["x0"]).astype(np.float64)
    if np.any(a != np.floor(a)): bad.append("whole numbers in x0")
    m = np.asarray(d["ml"]).astype(np.int64).reshape(N, 8, 16, C)
    if np.any(np.sort(m.reshape(N, 8, 16 * C), axis=-1) != np.minimum(np.arange(16 * C), W)): bad.append("every agent once in ml")
    if np.any((m[:, :, 1:] < W) & (m[:, :, :-1] >= W)): bad.append("members before empty slots in ml")
    l = np.asarray(d["lims"]).reshape(N, 8, 16, 2)
    if np.any(l != l[:, :, :1]): bad.append("lims alike in a group")
    return bad
def reference(x0, ac, ml, lims, wt):
    X = np.zeros((N, 8, W + 1, 16), np.int32)
    X[:, :, :W] = x0.astype(np.float32).astype(np.int32).reshape(N, 8, 16, W).transpose(0, 1, 3, 2)
    A = ac.reshape(N, 8, 16, H).transpose(0, 1, 3, 2); M = np.array(ml.reshape(N, 8, 16, C).transpose(0, 1, 3, 2))
    lim = lims.reshape(N, 8, 16, 2)[:, :, 0].astype(np.int64); wv = wt.reshape(N, 8, 16).astype(np.int64)
    G = np.arange(8)[:, None]; G3 = G[:, :, None]; low = np.tri(L, L, -1, dtype=bool); z = np.zeros(N, np.int64)
    for t in range(RO):
        cl = t & 3; lane = 4 * np.arange(L) + cl; M2 = M.copy(); X2 = X.copy(); z2 = np.zeros(N, np.int64); go = []
        for r in range(N):
            x, m, mb = X[r], M[r], owner(M[r])
            own = m[:, lane]; here = own < W; live = here[:, :, 0]; tx = x[G3, own]; U = np.max(tx, axis=2)
            gr = np.where(here, np.sum(U[:, :, None] - tx, axis=3), -1); s = pick(own, np.argmax(gr, axis=2)); xs = x[G, s]
            ds = np.where(here, np.sum((tx - xs[:, :, None]) ** 2, axis=3), -1)
            an = A[r][G, s & (H - 1)]; ad = mb[G3, an]; fit = live[:, :, None] & ((ad & 3) != cl); has = np.any(fit, axis=2)
            d = pick(ad, np.argmin(np.where(fit, np.sum((x[G3, an] - xs[:, :, None]) ** 2, axis=3), 2 ** 20), axis=2))
            first = ~np.any((d[:, :, None] == d[:, None, :]) & has[:, None, :] & low, axis=2)
            dm = m[G, d]; dh = dm < W; td = x[G3, dm]; V = np.maximum(U, np.max(td, axis=2))[:, :, None]
            worst = np.maximum(np.max(np.where(here, np.sum(V - tx, axis=3), 0), axis=2), np.max(np.where(dh, np.sum(V - td, axis=3), 0), axis=2))
            mer = has & first & (np.sum(here, axis=2) + np.sum(dh, axis=2) <= 16) & (worst <= lim[r, :, :1] + (z[r] & 15))
            want = live & ~mer & (np.max(gr, axis=2) > lim[r, :, 1:])
            xg = x[G, pick(own, np.argmax(ds, axis=2))]; away = here & (np.sum((tx - xg[:, :, None]) ** 2, axis=3) < ds)
            vacant = m[:, :, 0] >= W; free = np.argsort(~vacant, axis=1, kind="stable")
            k = np.add.accumulate(want.astype(np.int64), axis=1) - want.astype(np.int64)
            spl = want & (k < np.sum(vacant, axis=1)[:, None]); e = np.take_along_axis(free, k, 1)
            both = tight(np.concatenate([own, dm], axis=2))[:, :, :16]
            M2[r][:, lane] = np.where(mer[:, :, None], both, np.where(spl[:, :, None], tight(np.where(away, W, own)), own))
            a, b = np.nonzero(mer); M2[r][a, d[a, b]] = W
            a, b = np.nonzero(spl); M2[r][a, e[a, b]] = tight(np.where(away, own, W))[a, b]
            idle = live & ~mer & ~spl; a, b = np.nonzero(idle & (np.add.accumulate(idle.astype(np.int64), axis=1) <= CAP))
            go.append((a, s[a, b], xs[a, b])); z2[r] = np.sum(mer)
        for r in range(N):
            q = (r + 1 + t % (N - 1)) % N; a, sa, xa = go[r]
            v = np.sum(wv[q][a] * xa, axis=1) & (W - 1); mm = M2[q][a, owner(M2[q])[a, v]]; y = X[q][a[:, None], mm]
            j = np.argmin(np.where(mm < W, np.sum((y - xa[:, None]) ** 2, axis=2), 2 ** 20), axis=1)
            X2[r][a, sa] = (xa + y[np.arange(len(a)), j]) >> 1
        X, M, z = X2, M2, z2
    return {"ym": np.ascontiguousarray(M.transpose(0, 1, 3, 2)).reshape(N, 128, C).astype(np.float32),
            "yx": np.ascontiguousarray(X[:, :, :W].transpose(0, 1, 3, 2)).reshape(N, 128, W).astype(np.float32).astype(BF)}

@@ -1,0 +1,819 @@
+from concourse.mybir import AluOpType as O, ActivationFunctionType as AF, AxisListType as AX
+
+F4, B2, H2, I4, U2 = "float32", "bfloat16", "float16", "int32", "uint16"
+SCRATCH = {}
+for _n, _w, _d in [
+        ("xa", 2304, B2), ("xc", 2304, B2), ("xs", 2304, B2), ("ra", 2048, F4), ("rb", 2048, F4), ("r16", 2064, H2),
+        ("at", 2048, F4), ("bt", 1536, F4), ("sz", 1536, F4), ("el", 1280, F4), ("ks", 2080, F4),
+        ("gt", 3072, F4), ("g16", 2048, H2), ("df", 2048, B2), ("xr", 2048, B2), ("zb", 2048, B2), ("sqs", 2048, B2),
+        ("eq", 1024, B2), ("bw", 2048, B2), ("sets", 14336, H2), ("wts", 2048, B2), ("orp", 2048, H2),
+        ("mlt", 1024, I4), ("act", 1024, I4), ("d0", 1024, B2), ("ck16", 1024, H2),
+        ("mr", 1536, B2), ("ones", 512, B2), ("us", 2048, B2), ("rl", 2048, B2), ("m0", 2048, B2), ("rk", 2048, H2),
+        ("bt16", 1024, H2), ("xl", 1024, B2), ("xb", 1024, B2), ("wm", 4480, H2), ("wb", 1408, B2),
+        ("xsb", 256, B2), ("xbb", 256, B2), ("uc", 256, B2), ("ud", 256, B2), ("uv", 256, B2), ("acq", 256, U2), ("ai", 512, I4),
+        ("ahl", 512, F4), ("mrb", 512, B2), ("tg", 512, F4), ("tt", 512, F4),
+        ("ag16", 256, H2), ("eg16", 256, H2), ("drep", 256, H2), ("x16", 1024, H2), ("bl16", 256, H2), ("lt16", 256, H2),
+        ("dvt", 256, F4), ("lft", 256, F4), ("sze", 256, F4), ("zd", 256, F4), ("ctr", 256, F4),
+        ("vs", 352, B2), ("res", 352, B2), ("hx", 1536, B2), ("vag", 96, H2), ("yv", 96, B2), ("ri", 96, I4), ("nx", 256, B2),
+        ("sm", 2800, F4), ("si", 416, I4), ("su", 1120, U2), ("sh", 160, H2), ("sb", 160, B2), ("lim", 2, I4), ("wtc", 1, I4)]:
+    SCRATCH[_n] = ("sbuf", [128, _w], _d)
+for _t in range(4):
+    SCRATCH["in%d" % _t] = ("sbuf", [128, 96], B2)
+    SCRATCH["ry%d" % _t] = ("sbuf", [128, 96], B2)
+SCRATCH["psA"] = ("psum", [128, 2048], F4)
+SCRATCH["psB"] = ("psum", [128, 2048], F4)
+SEMAPHORES = ["sv", "ss", "st", "sg"] + ["d%d" % i for i in range(12)]
+for _t in range(4):
+    SEMAPHORES += ["ra%d" % _t, "rb%d" % _t, "la%d" % _t, "lb%d" % _t]
+BIG = 33554432.0
+
+
+def rank_program(g, core, T, topo):
+    rank = T.rank_of(core)
+    if rank is None:
+        return
+    Q = {"v": g.vector, "s": g.scalar, "t": g.tensor, "g": g, "y": g.sync}
+    SEM = {"v": "sv", "s": "ss", "t": "st", "g": "sg"}
+    cnt = {"v": 0, "s": 0, "t": 0, "g": 0}
+    know = {e: {} for e in Q}
+    hist = {}
+    recs = {}
+
+    def A(n, a=0, b=None, s=1):
+        return (n, a, SCRATCH[n][1][1] if b is None else b, s)
+
+    def X(w, o):
+        return ("X", w, o, 0)
+
+    def ap(x):
+        if not isinstance(x, tuple):
+            return x
+        if x[0] == "X":
+            return ap(x[1]).indirect(ap(x[2]))
+        n, a, b, s = x
+        return T[n][:, a:b] if s == 1 else T[n][:, a:b:s]
+
+    def sub(x, a, b, s=1):
+        return (x[0], x[1] + a, x[1] + b, s)
+
+    def touch(e, outs, ins, seq_e):
+        acc = []
+        for x, w in [(o, True) for o in outs] + [(i, False) for i in ins]:
+            if not isinstance(x, tuple):
+                continue
+            for y, ww in ([(x[1], w), (x[2], False)] if x[0] == "X" else [(x, w)]):
+                n, a, b, s = y
+                if n[:2] == "ps":
+                    for k in range(a // 512, (b - 1) // 512 + 1):
+                        acc.append((n, 512 * k, 512 * k + 512, True, True))
+                else:
+                    acc.append((n, a, b, ww, False))
+        need = {}
+        for n, a, b, w, ps in acc:
+            for r in recs.get(n, []):
+                if r[0] < b and a < r[1] and (w or r[4]) and not (r[2] == seq_e[0] and r[2][0] == "D") and not (ps and r[2] == e and e == "t"):
+                    need[r[2]] = max(need.get(r[2], 0), r[3])
+        for x in sorted(need):
+            if know[e].get(x, 0) < need[x]:
+                Q[e].wait_ge(T.sem[SEM[x]], need[x])
+                for k, v in hist[(x, need[x])].items():
+                    know[e][k] = max(know[e].get(k, 0), v)
+                know[e][x] = need[x]
+        who, seq = seq_e
+        hist[(who, seq)] = dict(know[e])
+        for n, a, b, w, ps in acc:
+            L = recs.setdefault(n, [])
+            if w:
+                L[:] = [r for r in L if not (a <= r[0] and r[1] <= b)]
+                L.append([a, b, who, seq, True])
+            else:
+                for r in L:
+                    if r[0] == a and r[1] == b and r[2] == who and not r[4]:
+                        r[3] = seq
+                        break
+                else:
+                    L.append([a, b, who, seq, False])
+
+    def emit(e, fn, outs, ins):
+        cnt[e] += 1
+        touch(e, outs, ins, (e, cnt[e]))
+        fn().then_inc(T.sem[SEM[e]], 1)
+
+    def cp(out, i, e="v"):
+        if e == "s":
+            act(out, i, AF.Copy)
+        else:
+            emit("v", lambda: g.vector.tensor_copy(ap(out), ap(i)), [out], [i])
+
+    def tt(out, a, b, op):
+        emit("v", lambda: g.vector.tensor_tensor(ap(out), ap(a), ap(b), op), [out], [a, b])
+
+    def ts(out, a, s1, op0, s2=None, op1=None):
+        if op1 is None:
+            emit("v", lambda: g.vector.tensor_scalar(ap(out), ap(a), ap(s1), None, op0), [out], [a, s1])
+        else:
+            emit("v", lambda: g.vector.tensor_scalar(ap(out), ap(a), ap(s1), ap(s2), op0, op1), [out], [a, s1, s2])
+
+    def scan(out, d0, d1, op0, op1):
+        emit("v", lambda: g.vector.tensor_tensor_scan(ap(out), ap(d0), ap(d1), 0.0, op0, op1), [out], [d0, d1])
+
+    def vtr(out, i):
+        emit("v", lambda: g.vector.transpose(ap(out), ap(i)), [out], [i])
+
+    def ms(out, c):
+        emit("v", lambda: g.vector.memset(ap(out), c), [out], [])
+
+    def act(out, i, f, scale=1.0):
+        emit("s", lambda: g.scalar.activation(ap(out), ap(i), f, scale=scale), [out], [i])
+
+    def mm(out, l, r, start=True, stop=True):
+        emit("t", lambda: g.tensor.matmul(ap(out), ap(l), ap(r), start, stop), [out], [l, r])
+
+    def mms(out, pairs):
+        for k, (l, r) in enumerate(pairs):
+            mm(out, l, r, k == 0, k == len(pairs) - 1)
+
+    def asel(out, i, pat, op, base, cm):
+        emit("g", lambda: g.affine_select(ap(out), ap(i), pat, op, 0.0, base, cm), [out], [i])
+
+    def iota(out, pat, base, cm):
+        emit("g", lambda: g.iota(ap(out), pat, base, cm, allow_small_or_imprecise_dtypes=True), [out], [])
+
+    nd = [0]
+
+    def dmas(e, pairs):
+        who = "D%d" % nd[0]
+        SEM[who] = "d%d" % nd[0]
+        nd[0] += 1
+        for k, (o, i, oa, ia) in enumerate(pairs):
+            touch(e, [o] if o else [], [i] if i else [], (who, 16 * len(pairs)))
+            Q[e].dma_start(oa, ia).then_inc(T.sem[SEM[who]], 16)
+        return who, 16 * len(pairs)
+
+    fin = []
+    slots = {}
+    used = {"sm": 0, "si": 0, "su": 0, "sh": 0, "sb": 0}
+
+    def S(buf, name, w=16):
+        if (buf, name) not in slots:
+            slots[(buf, name)] = A(buf, used[buf], used[buf] + w)
+            used[buf] += (w + 15) // 16 * 16
+        return slots[(buf, name)]
+
+    def F(name, w=16):
+        return S("sm", name, w)
+
+    for n, src in (("mlt", T.ml), ("xa", T.x0), ("act", T.ac), ("lim", T.lims), ("wtc", T.wt)):
+        w = src.shape[1]
+        fin.append(dmas("y" if n != "act" else "s", [(A(n, 0, w), None, T[n][:, 0:w], src[:, 0:w])]))
+
+    ms(A("ones"), 1.0)
+    ms(A("us"), 1.0)
+    iota(F("i16"), [[1, 16]], 0, 0)
+    iota(F("pi", 1), [[0, 1]], 0, 1)
+    asel(A("bw"), A("us"), [[1, 16], [0, 8], [-1, 16]], O.is_equal, 0, 0)
+    asel(A("bw"), A("bw"), [[0, 16], [-16, 8], [0, 16]], O.is_ge, 0, 1)
+    asel(A("bw"), A("bw"), [[0, 16], [16, 8], [0, 16]], O.is_ge, 15, -1)
+    wb = {}
+
+    def W1(name, buf="wb"):
+        k = (buf, name)
+        if k not in wb:
+            i = len([1 for z in wb if z[0] == buf])
+            wb[k] = A(buf, 128 * i, 128 * i + 128)
+        return wb[k]
+
+    o128 = A("ones", 0, 128)
+    BB, ID, SP, SN, TW = W1("BB"), W1("ID"), W1("SP"), W1("SN"), W1("TW")
+    asel(BB, o128, [[-16, 8], [0, 16]], O.is_ge, 0, 1)
+    asel(BB, BB, [[16, 8], [0, 16]], O.is_ge, 15, -1)
+    asel(ID, o128, [[-1, 128]], O.is_equal, 0, 1)
+    asel(SP, o128, [[-1, 128]], O.is_equal, 16, 1)
+    asel(SN, o128, [[-1, 128]], O.is_equal, -16, 1)
+    asel(TW, BB, [[1, 128]], O.is_gt, 0, -1)
+    cp1 = A("el", 0, 1024)
+    iota(cp1, [[1, 1024]], 1, 0)
+    iota(F("l16"), [[16, 16]], 0, 0)
+    iota(F("c64", 64), [[16, 64]], 0, 0)
+    m8 = A("tg", 384, 512)
+    iota(m8, [[1, 128]], 0, 0)
+    pi = S("si", "pi", 1)
+    kcol, mO, mE = F("kcol", 1), F("mO", 1), F("mE", 1)
+    cp(pi, F("pi", 1))
+    ts(S("si", "p2", 1), pi, 15, O.bitwise_and)
+    cp(kcol, S("si", "p2", 1))
+    ts(S("si", "p2", 1), pi, 4, O.arith_shift_right, 1, O.bitwise_and)
+    cp(mO, S("si", "p2", 1))
+    ts(mE, mO, -1.0, O.mult, 1.0, O.add)
+    ts(F("mE4", 1), mE, 4096.0, O.mult)
+    ts(F("mO4", 1), mO, 4096.0, O.mult)
+    ts(F("k128", 1), kcol, 128.0, O.mult)
+    ts(F("k11", 1), kcol, -11.0, O.add)
+    rm = F("rm")
+    ts(rm, F("i16"), kcol, O.is_equal)
+
+    def RM(r):
+        return sub(rm, r, r + 1)
+
+    def coef(name, terms):
+        c = F("c_" + name, 1)
+        r0, w0 = terms[0]
+        ts(c, RM(r0), float(w0), O.mult)
+        for r, w in terms[1:]:
+            ts(F("c_t", 1), RM(r), float(w), O.mult)
+            tt(c, c, F("c_t", 1), O.add)
+        return c
+
+    lane, c4 = F("lane"), F("c4", 64)
+    ts(lane, F("l16"), kcol, O.add)
+    ts(c4, F("c64", 64), kcol, O.add)
+    ts(S("sb", "tri"), F("i16"), kcol, O.is_gt)
+    ci, ck0, ck1 = A("ai"), A("ks", 0, 512), A("ks", 512, 1024)
+    for h in (0, 1):
+        cpart = A("el", 512 * h, 512 * h + 512)
+        ts(ck0, cpart, -1.0, O.add)
+        cp(ci, ck0)
+        ts(ci, ci, 3, O.bitwise_and)
+        ts(ck1, ci, F("k11", 1), O.is_equal)
+        ts(ck0, ck0, RM(8), O.mult)
+        tt(A("ck16", 512 * h, 512 * h + 512), ck0, ck1, O.add)
+    ts(A("d0"), A("us", 0, 1024), RM(2), O.mult)
+    names = ["E", "n", "r8", "cid", "P", "np", "st"]
+    terms = [[(2, 1), (3, -1), (6, 1), (7, 1)], [(7, 1)], [(8, 1)], [(1, 1)], [(0, 16), (10, 1)], [(2, 1), (3, -1), (5, 1)], [(2, 1), (3, -1), (6, 1)]]
+    ccol = {}
+
+    def setof(name):
+        i = names.index(name)
+        return lambda w: A("sets", 2048 * i + 128 * w, 2048 * i + 128 * w + 128)
+    for i, nm in enumerate(names):
+        ccol[nm] = coef(nm, terms[i])
+        ts(A("sets", 2048 * i, 2048 * i + 2048), A("bw"), ccol[nm], O.mult)
+    wf = F("wf", 1)
+    cp(wf, A("wtc"))
+    ts(A("wts"), A("bw"), wf, O.mult)
+
+    def bws(w):
+        return A("bw", 128 * w, 128 * w + 128)
+
+    s0s = setof("cid")
+
+    def wtw(w):
+        return A("wts", 128 * w, 128 * w + 128)
+
+    def ors(w):
+        return A("orp", 128 * w, 128 * w + 128)
+    for w in range(16):
+        ts(ors(w), BB, RM(w), O.mult)
+
+    def mk(name, src, col, w=1.0, buf="wm"):
+        m = W1(name, buf)
+        ts(m, src, col, O.mult, float(w), O.mult)
+        return m
+
+    one = F("one1", 1)
+    ms(one, 1.0)
+    I16 = mk("I16", ID, one)
+    PE_, PO_, P01, P10 = mk("PE", ID, mE), mk("PO", ID, mO), mk("P01", SP, mE), mk("P10", SN, mO)
+    BBK, BBS, BBN = mk("BBK", BB, one, 2048.0, "wb"), mk("BBS", BB, one, -8.0, "wb"), mk("BBN", BB, one, -1.0, "wb")
+    RKS, RKB = mk("RKS", BB, RM(0), -0.5), mk("RKB", BB, RM(0), -128.0)
+    BB16 = mk("BB16", BB, one)
+    RPS = mk("RPS", BB, coef("ks", [(0, 2.0 ** -8), (10, 2.0 ** -12), (9, 2048)]))
+    CDP, CDN = mk("CDP", BB, RM(1)), mk("CDN", BB, RM(1), -1.0)
+    STR, NRP = mk("STR", BB, ccol["st"]), mk("NRP", BB, ccol["n"])
+    CLS = [mk("CLS%d" % m, BB, RM(11 + m), 64.0) for m in range(4)]
+    mi = S("si", "mi", 128)
+    cp(mi, m8)
+    ts(mi, mi, 1, O.bitwise_and)
+    par = A("tg", 256, 384)
+    cp(par, mi)
+    RPB = W1("RPB", "wm")
+    ta, tb = A("tg", 0, 128), A("tg", 128, 256)
+    ts(ta, BB, coef("kb1", [(10, 1.0), (0, -1.0)]), O.mult)
+    tt(ta, ta, par, O.mult)
+    ts(tb, BB, coef("kb2", [(0, 1.0), (9, 2048.0)]), O.mult)
+    tt(RPB, ta, tb, O.add)
+
+    def rowmap(name, src, rows, w=1.0):
+        m = W1(name, "wm")
+        ts(ta, bws(rows[0]), RM(src), O.mult, float(w), O.mult)
+        for r in rows[1:]:
+            ts(tb, bws(r), RM(src), O.mult, float(w), O.mult)
+            tt(ta, ta, tb, O.add)
+        cp(m, ta)
+        return m
+    M237, M237N, M7N = rowmap("M237", 0, [2, 3, 7]), rowmap("M237N", 0, [2, 3, 7], -1), rowmap("M7N", 0, [7], -1)
+    M5, M1N, M81, M81N, M56 = rowmap("M5", 0, [5]), rowmap("M1N", 0, [1], -1), rowmap("M81", 8, [1]), rowmap("M81N", 8, [1], -1), rowmap("M56", 0, [5, 6])
+    M567 = W1("M567", "wm")
+    tt(M567, M7N, M56, O.add)
+    ts(M567, M567, -1.0, O.mult)
+    I23 = mk("I23", ID, coef("i23", [(2, 1), (3, 1)]))
+    IX = W1("IX", "wm")
+    tt(IX, I16, M81, O.add)
+    RPP = mk("RPP", BB, ccol["P"])
+    H0, PX10, H10, C1 = rowmap("H0", 0, [0]), W1("PX10", "wm"), rowmap("H10", 0, [10], -16), rowmap("C1", 0, [1])
+    cp(PX10, bws(10))
+    BB237 = W1("BB237", "wb")
+    tt(ta, bws(2), bws(3), O.add)
+    tt(BB237, ta, bws(7), O.add)
+    ms(A("mr"), 1.0)
+    ms(A("mr", 0, 1536, 16), 0.0)
+    ms(A("mrb"), 0.0)
+    ms(A("mrb", 0, 512, 16), BIG)
+    for n in ("zb", "eq", "xl", "xb"):
+        ms(A(n), 0.0)
+    ms(A("vs"), 0.0)
+    ms(A("zd"), 0.0)
+    ms(A("gt", 0, 2048), 0.0)
+    ms(F("neg"), -1.0)
+    cp(A("r16", 0, 16), F("neg"))
+    lims = F("lims", 2)
+    cp(lims, A("lim"))
+    limz = F("limz", 1)
+    cp(limz, sub(lims, 0, 1))
+
+    def gathO(src, a, n, st, out):
+        for w in range(16):
+            mm(out, st(w), A(src, a + w, a + n, 16), w == 0, w == 15)
+
+    def s2o(r1, out, n):
+        mms(sub(out, 0, n, 2), [(PE_, sub(r1, 0, n, 2)), (P01, sub(r1, 1, n, 2))])
+        mms(sub(out, 1, n, 2), [(P10, sub(r1, 0, n, 2)), (PO_, sub(r1, 1, n, 2))])
+
+    def lanes_of(win, dup):
+        cp(A("tg"), X(win, dup))
+        vtr(A("tt"), A("tg"))
+
+    def sel(out, r, me=mE, mo=mO):
+        ts(F("selA"), A("tt", r, 512, 32), me, O.mult)
+        ts(F("selB"), A("tt", 16 + r, 512, 32), mo, O.mult)
+        tt(out, F("selA"), F("selB"), O.add)
+
+    def prefix(ind, n, out, tag, ps):
+        mm(sub(ps, 0, n), TW, ind)
+        mm(sub(ps, n, 2 * n), BB, ind)
+        cp(F(tag + "tot", n), sub(ps, n, 2 * n))
+        inc = F(tag + "inc", n)
+        scan(inc, A("ones", 0, n), F(tag + "tot", n), O.mult, O.add)
+        tt(out, inc, F(tag + "tot", n), O.subtract)
+        tt(out, out, sub(ps, 0, n), O.add)
+        return sub(inc, n - 1, n)
+
+    def lt(name):
+        return F(name)
+
+    def choose(out, cond, a, b, tmp="chT", w=16):
+        d = F(tmp + str(w), w)
+        tt(d, a, b, O.subtract)
+        tt(d, d, cond, O.mult)
+        tt(out, d, b, O.add)
+
+    B0, B1, B2_, B3 = [A("psB", 512 * k, 512 * k + 512) for k in range(4)]
+    PO, CQ, CQF = S("su", "po", 128), S("su", "cq", 128), F("cqf", 128)
+
+    def chunks(off, k, n):
+        w = (off[2] - off[1]) // n
+        return sub(off, k * w, k * w + w)
+
+    def order_tables(R):
+        for k in range(4):
+            act(A("r16", 16 + 512 * k, 528 + 512 * k), A(R, 512 * k, 512 * k + 512), AF.Copy)
+        gathO("r16", 16, 2048, setof("P"), sub(B1, 0, 128))
+        gathO("r16", 16, 2048, setof("cid"), sub(B2_, 0, 128))
+        cp(PO, sub(B1, 0, 128))
+        cp(CQF, sub(B2_, 0, 128))
+        cp(CQ, CQF)
+        for k in range(4):
+            mms(A("psA", 512 * k, 512 * k + 512), [(CDP, A("r16", 16 + 512 * k, 528 + 512 * k)), (CDN, A("r16", 15 + 512 * k, 527 + 512 * k))])
+            ts(A("m0", 512 * k, 512 * k + 512), A("psA", 512 * k, 512 * k + 512), 0.0, O.is_equal)
+        scan(A("rk"), A("m0"), A("m0"), O.mult, O.add)
+
+    def gather_xs():
+        for k in range(4):
+            act(A("xs", 512 * k, 512 * k + 512), X(A("xa", 0, 2048), chunks(PO, k, 4)), AF.Copy)
+
+    def agents(POx):
+        cp(X(A("at"), POx), A("gt", 0, 2048))
+
+    def build_xc(m):
+        act(A("g16"), A("at"), AF.Copy)
+        for k in range(4):
+            c = A("psA", 512 * k, 512 * k + 512)
+            mms(c, [(ID, A("xa", 512 * k, 512 * k + 512)), (CLS[m], A("g16", 512 * k, 512 * k + 512))])
+            act(A("xc", 512 * k, 512 * k + 512), c, AF.Copy)
+
+    ts(A("us", 0, 1024), A("mlt"), 2048.0, O.is_lt)
+    for k in range(2):
+        mms(A("psB", 512 * k, 512 * k + 512), [(BB237, A("us", 512 * k, 512 * k + 512)), (I16, A("ck16", 512 * k, 512 * k + 512))])
+    cp(A("sz", 0, 1024), A("psB", 0, 1024))
+    scan(A("bt", 0, 1024), A("d0"), A("sz", 0, 1024), O.mult, O.add)
+    cp(A("bt16"), A("bt", 0, 1024))
+    cp(A("lt16"), A("bt", 0, 1024, 4))
+    gathO("bt16", 0, 1024, setof("np"), sub(B2_, 0, 64))
+    gathO("bt16", 0, 1024, setof("n"), sub(B2_, 64, 128))
+    t64, u64 = F("t64", 64), F("u64", 64)
+    ts(t64, c4, 2048.0, O.add)
+    ts(u64, sub(B2_, 64, 128), 0.5, O.is_gt)
+    s64 = F("s64", 64)
+    cp(s64, sub(B2_, 0, 64))
+    choose(s64, u64, s64, t64, "ch64", 64)
+    cp(S("su", "l64", 64), s64)
+    cp(X(A("gt"), S("su", "l64", 64)), cp1)
+    ts(A("m0"), A("gt", 0, 2048), 0.0, O.is_equal)
+    scan(A("ks", 0, 2048), A("m0"), A("gt", 0, 2048), O.mult, O.add)
+    ts(A("g16"), A("ks", 0, 2048), -1.0, O.add)
+    ms(A("el"), 0.0)
+    gathO("g16", 0, 2048, s0s, sub(B2_, 0, 128))
+    cp(CQF, sub(B2_, 0, 128))
+    cp(CQ, CQF)
+    scan(A("rk"), A("m0"), A("m0"), O.mult, O.add)
+    ts(A("rl"), A("rk"), kcol, O.is_equal)
+    for k in range(4):
+        c = (512 * k, 512 * k + 512)
+        px = A("r16", 16 + 512 * k, 528 + 512 * k)
+        tt(px, X(A("mlt"), chunks(CQ, k, 4)), A("rl", *c), O.mult)
+        mm(A("psA", *c), BB16, px)
+        ts(A("ai"), A("psA", *c), 0.0625, O.mult, -0.46875, O.add)
+        cp(A("bt16", 0, 512), A("ai"))
+        mms(A("psB", *c), [(H0, A("bt16", 0, 512)), (PX10, px), (H10, A("bt16", 0, 512)), (C1, A("g16", *c))])
+        ts(A("ra", *c), A("psB", *c), RM(9), O.add)
+    for k in range(4):
+        act(A("r16", 16 + 512 * k, 528 + 512 * k), A("ra", 512 * k, 512 * k + 512), AF.Copy)
+    gathO("r16", 16, 2048, setof("P"), sub(B1, 0, 128))
+    cp(PO, sub(B1, 0, 128))
+    for k in range(4):
+        act(A("gt", 512 * k, 512 * k + 512), X(A("bt", 0, 1024), chunks(CQ, k, 4)), AF.Copy)
+    agents(PO)
+    gather_xs()
+    build_xc(0)
+    R = ["ra", "rb"]
+
+    for t in range(4):
+        cl = t
+        lanes = (cl, 1024, 4)
+        gathO("lt16", 0, 256, setof("E"), sub(B1, 0, 16))
+        gathO("lt16", 0, 256, setof("n"), sub(B1, 16, 32))
+        EU, ED2 = S("su", "eu"), S("su", "ed2", 32)
+        nc = F("nc")
+        for o in (EU, sub(ED2, 0, 32, 2), sub(ED2, 1, 32, 2)):
+            ts(o, sub(B1, 0, 16), -1.0, O.add)
+        cp(nc, sub(B1, 16, 32))
+        scan(A("us"), A("m0"), A("xs", 0, 2048), O.mult, O.max)
+        for k in range(4):
+            c = (512 * k, 512 * k + 512)
+            mms(A("psA", *c), [(RKS, A("rk", *c)), (RPS, A("r16", 16 + 512 * k, 528 + 512 * k)), (BBS, A("xs", *c))])
+        scan(A("ks", 0, 2048), A("m0"), A("psA"), O.mult, O.max)
+        lanes_of(A("ks", 0, 2048), ED2)
+        sel(F("key"), 0, F("mE4", 1), F("mO4", 1))
+        ki, k2 = S("si", "ki"), S("si", "k2")
+        sf, hf, sig, rnk = F("sf"), F("hf"), F("sig"), F("rnk")
+        cp(ki, F("key"))
+        ts(k2, ki, 2047, O.bitwise_and)
+        cp(sf, k2)
+        cp(S("su", "sU"), k2)
+        ts(k2, ki, 1023, O.bitwise_and)
+        cp(S("su", "hU"), k2)
+        cp(A("acq"), X(A("act"), S("su", "hU")))
+        cp(A("xsb"), X(A("xa", 0, 2048), S("su", "sU")))
+        for k in range(4):
+            z0 = 1024 * (k % 2)
+            c = (z0, z0 + 1024)
+            cp(A("zb", z0, z0 + 1024, 16), A("xsb", 64 * k, 64 * k + 64))
+            scan(A("xr", *c), A("mr", 0, 1024), A("zb", *c), O.mult, O.add)
+            tt(A("df", *c), X(A("xc", 0, 2048), A("acq", 64 * k, 64 * k + 64)), A("xr", *c), O.subtract)
+            act(A("df", *c), A("df", *c), AF.Square)
+            for i in range(16):
+                mm(A("psB", 64 * k, 64 * k + 64), bws(i), A("df", z0 + i, z0 + 1024, 16), i == 0, i == 15)
+        cp(A("xl", *lanes), A("xsb"))
+        for k in range(4):
+            c = (512 * k, 512 * k + 512)
+            hc = A("hx", 512 * (k % 2), 512 * (k % 2) + 512)
+            tt(hc, X(A("xl"), chunks(CQ, k, 4)), A("xs", *c), O.subtract)
+            act(A("sqs", *c), hc, AF.Square)
+            mms(A("psA", *c), [(RKB, A("rk", *c)), (RPB, A("r16", 16 + 512 * k, 528 + 512 * k)), (BBK, A("sqs", *c))])
+        ts(k2, ki, 11, O.arith_shift_right)
+        ts(F("y"), k2, -1.0, O.mult, 4096.0, O.add)
+        cp(ki, F("y"))
+        ts(k2, ki, 4, O.arith_shift_right)
+        cp(sig, k2)
+        ts(k2, ki, 15, O.bitwise_and)
+        cp(rnk, k2)
+        cp(A("uc"), X(A("us"), EU))
+        for w in range(16):
+            mm(sub(B1, 32, 48), bws(w), A("uc", w, 256, 16), w == 0, w == 15)
+        gr, live, want0 = F("gr"), F("live"), F("want0")
+        tt(gr, sub(B1, 32, 48), sig, O.subtract)
+        ts(live, nc, 0.5, O.is_gt)
+        ts(want0, gr, sub(lims, 1, 2), O.is_gt)
+        tt(want0, want0, live, O.mult)
+        act(A("bt16"), A("sz", 0, 1024), AF.Copy)
+        gathO("bt16", 0, 1024, setof("n"), sub(B2_, 0, 64))
+        e64, r64 = F("e64", 64), F("r64", 64)
+        ts(e64, sub(B2_, 0, 64), 0.5, O.is_lt)
+        cp(S("sb", "e64", 64), e64)
+        ecnt = prefix(S("sb", "e64", 64), 64, r64, "pe", sub(B2_, 64, 192))
+        ts(F("t64", 64), c4, 256.0, O.add)
+        ts(F("u64", 64), r64, 255.5, O.is_lt)
+        tt(e64, e64, F("u64", 64), O.mult)
+        choose(r64, e64, r64, F("t64", 64), "ch64", 64)
+        cp(S("su", "l64", 64), r64)
+        cp(X(A("el"), S("su", "l64", 64)), A("ck16"))
+        ai0, ai1 = A("ai", 0, 256), A("ai", 256, 512)
+        cp(ai0, A("acq"))
+        ts(ai1, ai0, 15, O.bitwise_and)
+        ts(ai0, ai0, 4, O.arith_shift_right)
+        ts(A("ahl"), A("ai"), F("k128", 1), O.add, 1.0 / 2048, O.mult)
+        for h in (0, 1):
+            tt(A("tg", 256 * h, 256 * h + 256), sub(B0, 0, 256), A("ahl", 256 * h, 256 * h + 256), O.add)
+        vtr(A("tt"), A("tg"))
+        scan(A("tg"), A("mrb"), A("tt"), O.max, O.min)
+        r32 = S("si", "r32", 32)
+        ts(r32, A("tg", 15, 512, 16), 2048.0, O.mult)
+        ts(S("si", "rh"), sub(r32, 0, 16), 127, O.bitwise_and)
+        ts(S("si", "rl"), sub(r32, 16, 32), 15, O.bitwise_and)
+        ts(F("ah"), S("si", "rh"), 16.0, O.mult, -2048.0, O.add)
+        tt(F("ah"), F("ah"), S("si", "rl"), O.add)
+        ts(F("fit"), A("tg", 15, 256, 16), 4096.0, O.is_lt)
+        tt(F("ah"), F("ah"), F("fit"), O.mult)
+        ts(S("sh", "a16"), F("ah"), 2048.0, O.add)
+        s2o(S("sh", "a16"), sub(B1, 48, 64), 16)
+        has = F("has")
+        ts(has, sub(B1, 48, 64), 2047.5, O.is_lt)
+        tt(has, has, live, O.mult)
+        ts(S("su", "aU"), sub(B1, 48, 64), 2047.0, O.min)
+        cp(A("ag16"), X(A("at"), S("su", "aU")))
+        gathO("ag16", 0, 256, setof("E"), sub(B1, 64, 80))
+        gathO("ag16", 0, 256, setof("r8"), sub(B1, 80, 96))
+        gathO("ag16", 0, 256, setof("n"), sub(B1, 96, 112))
+        DU, DD2 = S("su", "du"), S("su", "dd2", 32)
+        for o in (DU, sub(DD2, 0, 32, 2), sub(DD2, 1, 32, 2)):
+            ts(o, sub(B1, 64, 80), -1.0, O.add)
+        dn, df_, d47 = F("dn"), F("d"), F("d47")
+        cp(dn, sub(B1, 96, 112))
+        cp(df_, sub(B1, 80, 96))
+        ts(d47, df_, -2047.0, O.add)
+        tt(d47, d47, has, O.mult)
+        ts(d47, d47, 2047.0, O.add)
+        cp(S("sh", "d16"), d47)
+        for w in range(16):
+            mm(sub(B3, w, 256, 16), ors(w), S("sh", "d16"))
+        cp(A("drep"), sub(B3, 0, 256), "v")
+        cp(A("ud"), X(A("us"), DU))
+        tt(A("uv"), A("uc"), A("ud"), O.max)
+        for w in range(16):
+            mm(sub(B1, 112, 128), bws(w), A("uv", w, 256, 16), w == 0, w == 15)
+        for u in range(16):
+            q0 = 256 * (u % 4)
+            if u % 4 == u:
+                if u:
+                    ms(A("eq", q0, q0 + 16 * u), 0.0)
+            else:
+                ms(A("eq", q0 + 16 * (u - 4), q0 + 16 * u), 0.0)
+            ts(A("eq", q0 + 16 * u, q0 + 256), A("drep", 16 * u, 256), sub(d47, u, u + 1), O.is_equal)
+            tt(A("eq", q0 + 16 * u, q0 + 16 * u + 16), A("eq", q0 + 16 * u, q0 + 16 * u + 16), S("sb", "tri"), O.mult)
+            mm(sub(B3, 256, 512), BB, A("eq", q0, q0 + 256), u == 0, u == 15)
+        lanes_of(A("ks", 0, 2048), DD2)
+        sel(F("key"), 0, F("mE4", 1), F("mO4", 1))
+        cp(ki, F("key"))
+        ts(k2, ki, 11, O.arith_shift_right)
+        ts(F("y"), k2, -1.0, O.mult, 4096.0, O.add)
+        cp(ki, F("y"))
+        ts(k2, ki, 4, O.arith_shift_right)
+        cp(F("sigd"), k2)
+        mer, tmp = F("mer"), F("tmp")
+        tt(tmp, F("sigd"), sig, O.min)
+        tt(tmp, sub(B1, 112, 128), tmp, O.subtract)
+        ts(mer, tmp, limz, O.is_le)
+        tt(tmp, nc, dn, O.add)
+        ts(tmp, tmp, 16.5, O.is_lt)
+        tt(mer, mer, tmp, O.mult)
+        tt(mer, mer, has, O.mult)
+        vtr(A("ctr"), sub(B3, 256, 512))
+        cp(S("sh", "ct"), A("ctr", 0, 256, 16))
+        s2o(S("sh", "ct"), sub(B1, 128, 144), 16)
+        ts(tmp, sub(B1, 128, 144), 0.5, O.is_lt)
+        tt(mer, mer, tmp, O.mult)
+        want, spl, wk = F("want"), F("spl"), F("wk")
+        ts(tmp, mer, -1.0, O.mult, 1.0, O.add)
+        tt(want, want0, tmp, O.mult)
+        cp(S("sb", "wb"), want)
+        prefix(S("sb", "wb"), 16, wk, "pw", sub(B1, 144, 176))
+        ts(tmp, wk, ecnt, O.is_lt)
+        tt(spl, want, tmp, O.mult)
+        cp(S("su", "kU"), wk)
+        cp(A("eg16"), X(A("el"), S("su", "kU")))
+        scan(A("gt", 0, 2048), A("m0"), A("psA"), O.mult, O.max)
+        lanes_of(A("gt", 0, 2048), ED2)
+        sel(F("kb0"), 0)
+        sel(F("kb1"), 1)
+        cp(ki, F("kb0"))
+        ts(ki, ki, 127, O.bitwise_and)
+        cp(k2, F("kb1"))
+        ts(k2, k2, 15, O.bitwise_and)
+        bf = F("bf")
+        ts(bf, ki, 16.0, O.mult)
+        tt(bf, bf, k2, O.add)
+        choose(bf, spl, bf, sf)
+        cp(S("su", "bU"), bf)
+        cp(A("xbb"), X(A("xa", 0, 2048), S("su", "bU")))
+        cp(A("xb", *lanes), A("xbb"))
+        for k in range(4):
+            c = (512 * k, 512 * k + 512)
+            hc = A("hx", 512 * (k % 2), 512 * (k % 2) + 512)
+            tt(hc, X(A("xb"), chunks(CQ, k, 4)), A("xs", *c), O.subtract)
+            act(hc, hc, AF.Square)
+            mms(A("psA", *c), [(BB, hc), (BBN, A("sqs", *c))])
+            ts(A("g16", *c), A("psA", *c), 0.0, O.is_lt)
+        cp(A("xb", *lanes), A("xsb"))
+        scan(A("rl"), A("m0"), A("g16"), O.mult, O.add)
+        for src, o, st in (("g16", 0, s0s), ("rl", 128, bws), ("rk", 256, s0s)):
+            gathO(src, 0, 2048, st, sub(B2_, o, o + 128))
+        lanes_of(A("rl"), ED2)
+        nl = F("nl")
+        sel(nl, 0)
+        tt(nl, nl, spl, O.mult)
+        gathO("eg16", 0, 256, setof("r8"), sub(B1, 176, 192))
+        tl = F("tl")
+        ts(tl, lane, 1280.0, O.add)
+        choose(tmp, spl, sub(B1, 176, 192), tl)
+        cp(S("su", "eL"), tmp)
+        choose(tmp, mer, df_, tl)
+        cp(S("su", "dL"), tmp)
+        x1 = S("sh", "x1", 64)
+        tt(tmp, mer, dn, O.mult)
+        tt(sub(x1, 0, 16), nc, tmp, O.add)
+        cp(sub(x1, 16, 32), nl)
+        cp(sub(x1, 32, 48), nc)
+        cp(sub(x1, 48, 64), df_)
+        for w in range(16):
+            for h in (0, 1):
+                mm(A("psA", 512 * h + w, 512 * h + 512, 16), ors(w), sub(x1, 32 * h, 32 * h + 32))
+        act(A("x16"), A("psA", 0, 1024), AF.Copy)
+        xr_, xl_, xn_, xd_ = [A("x16", 256 * k, 256 * k + 256) for k in range(4)]
+        ckl = A("ck16", cl, 1024, 4)
+        p0, p1 = sub(B0, 0, 256), sub(B0, 256, 512)
+        mms(p0, [(M237, xr_), (M7N, xl_), (I16, ckl)])
+        mms(p1, [(M237, xl_), (I16, A("eg16"))])
+        cp(A("sz", cl, 1024, 4), p0)
+        cp(X(A("sz"), S("su", "dL")), A("zd"))
+        scan(A("bt", 0, 1024), A("d0"), A("sz", 0, 1024), O.mult, O.add)
+        cp(A("bl16"), A("bt", cl, 1024, 4))
+        cp(A("sze"), p1)
+        mms(p0, [(I16, A("bl16")), (M5, xn_), (M1N, xd_), (M81, ckl)])
+        mms(p1, [(I23, A("bl16")), (M56, xn_), (M567, xl_), (IX, A("eg16")), (M81N, ckl)])
+        gathO("bl16", 0, 256, setof("np"), sub(B1, 192, 208))
+        cp(A("dvt"), p0)
+        cp(A("bt", 1024, 1280), p1)
+        cp(A("lft"), p1)
+        p2 = sub(B3, 0, 256)
+        mms(p2, [(M237, xr_), (M237N, xl_), (I16, ckl)])
+        cp(X(A("bt"), S("su", "eL")), A("lft"))
+        if t < 3:
+            cp(A("lt16"), A("bt", cl + 1, 1024, 4))
+        else:
+            cp(A("bt16"), A("bt", 0, 1024))
+        cp(X(A("bt"), S("su", "dL")), A("dvt"))
+        cp(A("sz", cl, 1024, 4), p2)
+        cp(X(A("sz"), S("su", "eL")), A("sze"))
+        stc = F("stc")
+        cp(stc, sub(B1, 192, 208))
+        cv, lv, cql, rp = F("cv", 128), F("lv", 128), F("cql", 128), F("rp", 128)
+        cp(lv, sub(B2_, 0, 128))
+        ts(cv, CQF, -0.75, O.mult, 1024.0 - cl / 4.0, O.add)
+        tt(cv, cv, lv, O.mult)
+        tt(cql, cv, CQF, O.add)
+        cp(S("su", "cqL", 128), cql)
+        for k in range(4):
+            c = (512 * k, 512 * k + 512)
+            act(A("gt", *c), X(A("bt", 0, 1280), chunks(S("su", "cqL", 128), k, 4)), AF.Copy)
+            act(A("g16", *c), A("gt", *c), AF.Copy)
+        gathO("g16", 0, 2048, setof("np"), sub(B3, 256, 384))
+        rkO, rlO = F("rkO", 128), F("rlO", 128)
+        cp(rkO, sub(B2_, 256, 384))
+        ts(rlO, sub(B2_, 128, 256), 0.0625, O.mult)
+        tt(rp, rkO, rlO, O.subtract)
+        tt(rlO, rlO, rp, O.subtract)
+        ts(rlO, rlO, -1.0, O.add)
+        tt(rlO, rlO, lv, O.mult)
+        tt(rp, rp, rlO, O.add)
+        tt(rp, rp, sub(B3, 256, 384), O.add)
+        cp(S("su", "npL", 128), rp)
+        tt(X(A(R[1]), S("su", "npL", 128)), A("gt", 0, 2048), A(R[0]), O.add)
+        R = R[::-1]
+        agents(PO)
+        order_tables(R[0])
+        gather_xs()
+        idle, visit, vk = F("idle"), F("visit"), F("vk")
+        tt(tmp, mer, spl, O.add)
+        tt(idle, live, tmp, O.subtract)
+        cp(S("sb", "ib"), idle)
+        prefix(S("sb", "ib"), 16, vk, "pv", sub(B1, 208, 240))
+        ts(visit, vk, 95.5, O.is_lt)
+        tt(visit, visit, idle, O.mult)
+        ts(tl, lane, 96.0, O.add)
+        choose(tmp, visit, vk, tl)
+        cp(S("su", "vL"), tmp)
+        cp(X(A("vs"), S("su", "vL")), A("xsb"))
+        ts(tl, lane, 2048.0, O.add)
+        choose(tmp, visit, sf, tl)
+        cp(S("su", "vA"), tmp)
+        tt(stc, stc, rnk, O.add)
+        choose(tmp, visit, stc, tl)
+        cp(S("su", "vP"), tmp)
+        q = T.cores[(rank + 1 + t % 7) % 8]
+        h = T.cores[(rank - 1 - t % 7) % 8]
+
+        def send(dst, out, src, rs, ls):
+            rid, pid, _ = topo.addr(dst)
+            es = topo.engines(core, dst)[:4]
+            m = 0
+            for e in es:
+                m |= 1 << e
+            SEM[ls] = ls
+            touch("g", [], [src], (ls, len(es)))
+            g.remote_dma(out_ap=T[out][:], in_ap=ap(src), remote_sem=T.sem[rs], local_sem=T.sem[ls], pid=pid, routing_id=rid, dma_engine_mask=m)
+            fin.append((ls, len(es)))
+
+        def arrived(buf, rs, src):
+            n = len(topo.engines(src, core)[:4])
+            SEM[rs] = rs
+            hist[(rs, n)] = {}
+            recs.setdefault(buf, []).append([0, 96, rs, n, True])
+            fin.append((rs, n))
+
+        send(q, "in%d" % t, A("vs", 0, 96), "ra%d" % t, "la%d" % t)
+        if t < 3:
+            mt = S("sb", "mt")
+            cp(mt, mer)
+            mm(sub(B1, 240, 256), o128, mt)
+            emit("v", lambda: g.vector.tensor_reduce(ap(F("zz", 1)), ap(sub(B1, 240, 256)), AX.X, O.add), [F("zz", 1)], [sub(B1, 240, 256)])
+            zi = S("si", "zi", 1)
+            cp(zi, F("zz", 1))
+            ts(zi, zi, 15, O.bitwise_and)
+            tt(limz, sub(lims, 0, 1), zi, O.add)
+            build_xc(cl + 1)
+        arrived("in%d" % t, "ra%d" % t, h)
+        IN = "in%d" % t
+        for w in range(16):
+            mm(sub(B1, 256, 262), wtw(w), A(IN, w, 96, 16), w == 0, w == 15)
+        vi = S("si", "vi", 6)
+        cp(vi, sub(B1, 256, 262))
+        ts(vi, vi, 2047, O.bitwise_and)
+        cp(S("su", "vi", 6), vi)
+        cp(A("vag"), X(A("at"), S("su", "vi", 6)))
+        mm(sub(B1, 272, 368), STR, A("vag"))
+        mm(sub(B1, 368, 464), NRP, A("vag"))
+        hl = F("hl", 96)
+        ts(hl, sub(B1, 368, 464), -1.0, O.add, kcol, O.min)
+        tt(hl, hl, sub(B1, 272, 368), O.add)
+        cp(S("su", "hl", 96), hl)
+        cp(A("zb", 0, 1536, 16), A(IN))
+        scan(A("xr", 0, 1536), A("mr", 0, 1536), A("zb", 0, 1536), O.mult, O.add)
+        tt(A("hx"), X(A("xs", 0, 2048), S("su", "hl", 96)), A("xr", 0, 1536), O.subtract)
+        act(A("hx"), A("hx"), AF.Square)
+        for i in range(16):
+            mm(sub(B0, 0, 96), bws(i), A("hx", i, 1536, 16), i == 0, i == 15)
+        ts(A("tg", 0, 96), sub(B0, 0, 96), 16.0, O.mult, kcol, O.add)
+        vtr(A("tt", 0, 96), A("tg", 0, 96))
+        scan(A("tg", 0, 96), A("mrb", 0, 96), A("tt", 0, 96), O.max, O.min)
+        k6 = S("si", "k6", 6)
+        cp(k6, A("tg", 15, 96, 16))
+        ts(k6, k6, 15, O.bitwise_and)
+        cp(S("sh", "k6", 6), k6)
+        s2o(S("sh", "k6", 6), sub(B1, 464, 470), 6)
+        for w in range(16):
+            mm(sub(B2_, 384, 390), setof("st")(w), A("vag", w, 96, 16), w == 0, w == 15)
+        y6 = F("y6", 6)
+        cp(y6, sub(B1, 464, 470))
+        tt(y6, y6, sub(B2_, 384, 390), O.add)
+        cp(S("su", "y6", 6), y6)
+        cp(A("yv"), X(A("xs", 0, 2048), S("su", "y6", 6)))
+        send(h, "ry%d" % t, A("yv"), "rb%d" % t, "lb%d" % t)
+        arrived("ry%d" % t, "rb%d" % t, q)
+        tt(A("ri"), A("ry%d" % t), A("vs", 0, 96), O.add)
+        ts(A("ri"), A("ri"), 1, O.arith_shift_right)
+        cp(A("res", 0, 96), A("ri"))
+        cp(A("res", 96, 352), A("xsb"))
+        cp(A("nx"), X(A("res"), S("su", "vL")))
+        cp(X(A("xa"), S("su", "vA")), A("nx"))
+        if t < 3:
+            cp(X(A("xc"), S("su", "vA")), A("nx"))
+            cp(X(A("xs"), S("su", "vP")), A("nx"))
+    fin.append(dmas("y", [(None, A("xa", 0, 2048), T.yx[:, 0:2048], T["xa"][:, 0:2048])]))
+    for k in range(4):
+        mm(A("psA", 512 * k, 512 * k + 512), RPP, A("r16", 16 + 512 * k, 528 + 512 * k))
+        act(A("ks", 512 * k, 512 * k + 512), A("psA", 512 * k, 512 * k + 512), AF.Copy)
+    ms(A("ks", 2048, 2080), 2048.0)
+    fin.append(dmas("y", [(A("gt", 0, 2048), A("ks"), T["gt"][k::16, 0:2048], T["ks"][k::16, k:k + 2048]) for k in range(16)]))
+    gathO("bt16", 0, 1024, setof("st"), sub(B2_, 0, 64))
+    ts(S("su", "l64", 64), sub(B2_, 0, 64), 2047.0, O.min)
+    for k in range(2):
+        mm(A("psB", 512 * k, 512 * k + 512), NRP, A("bt16", 512 * k, 512 * k + 512))
+    ye, yb = A("el", 0, 1024), A("bt", 0, 1024)
+    ts(yb, A("psB", 0, 1024), kcol, O.is_gt)
+    cp(ye, X(A("gt", 0, 2048), S("su", "l64", 64)))
+    ts(ye, ye, -2048.0, O.add)
+    tt(ye, ye, yb, O.mult)
+    ts(ye, ye, 2048.0, O.add)
+    fin.append(dmas("y", [(None, ye, T.ym[:, 0:1024], T["el"][:, 0:1024])]))
+    for who, v in fin + [(e, cnt[e]) for e in ("v", "s", "t", "g")]:
+        g.wait_ge(T.sem[SEM[who]], v)

@@ -4,18 +4,18 @@ F4, B2, H2, I4, U2 = "float32", "bfloat16", "float16", "int32", "uint16"
 SCRATCH = {}
 for _n, _w, _d in [
         ("xa", 2304, B2), ("xc", 2304, B2), ("xs", 2304, B2), ("ra", 2048, F4), ("rb", 2048, F4), ("r16", 2064, H2),
-        ("at", 2048, F4), ("bt", 1536, F4), ("sz", 1536, F4), ("el", 1280, F4), ("ks", 2080, F4),
-        ("gt", 3072, F4), ("g16", 2048, H2), ("df", 2048, B2), ("xr", 2048, B2), ("zb", 2048, B2), ("sqs", 2048, B2),
+        ("at", 2048, F4), ("bt", 1536, F4), ("sz", 1536, F4), ("el", 1280, F4), ("ks", 4128, F4),
+        ("gt", 2048, F4), ("g16", 2048, H2), ("df", 2048, B2), ("xr", 2048, B2), ("zb", 2048, B2), ("sqs", 2048, B2),
         ("eq", 1024, B2), ("bw", 2048, B2), ("sets", 14336, H2), ("wts", 2048, B2), ("orp", 2048, H2),
         ("mlt", 1024, I4), ("act", 1024, I4), ("d0", 1024, B2), ("ck16", 1024, H2),
         ("mr", 1536, B2), ("ones", 512, B2), ("us", 2048, B2), ("rl", 2048, B2), ("m0", 2048, B2), ("rk", 2048, H2),
-        ("bt16", 1024, H2), ("xl", 1024, B2), ("xb", 1024, B2), ("wm", 4480, H2), ("wb", 1408, B2),
+        ("bt16", 1024, H2), ("xl", 1024, B2), ("xb", 1024, B2), ("wm", 3968, H2), ("wb", 1664, B2),
         ("xsb", 256, B2), ("xbb", 256, B2), ("uc", 256, B2), ("ud", 256, B2), ("uv", 256, B2), ("acq", 256, U2), ("ai", 512, I4),
         ("ahl", 512, F4), ("mrb", 512, B2), ("tg", 512, F4), ("tt", 512, F4),
         ("ag16", 256, H2), ("eg16", 256, H2), ("drep", 256, H2), ("x16", 1024, H2), ("bl16", 256, H2), ("lt16", 256, H2),
         ("dvt", 256, F4), ("lft", 256, F4), ("sze", 256, F4), ("zd", 256, F4), ("ctr", 256, F4),
-        ("vs", 352, B2), ("res", 352, B2), ("hx", 1536, B2), ("vag", 96, H2), ("yv", 96, B2), ("ri", 96, I4), ("nx", 256, B2),
-        ("sm", 2800, F4), ("si", 416, I4), ("su", 1120, U2), ("sh", 160, H2), ("sb", 160, B2), ("lim", 2, I4), ("wtc", 1, I4)]:
+        ("vs", 352, B2), ("res", 352, B2), ("vag", 96, H2), ("yv", 96, B2), ("ri", 96, I4), ("nx", 256, B2),
+        ("sm", 2800, F4), ("si", 416, I4), ("su", 1120, U2), ("sh", 288, H2), ("sb", 160, B2), ("lim", 2, I4), ("wtc", 1, I4)]:
     SCRATCH[_n] = ("sbuf", [128, _w], _d)
 for _t in range(4):
     SCRATCH["in%d" % _t] = ("sbuf", [128, 96], B2)
@@ -124,7 +124,7 @@ def rank_program(g, core, T, topo):
         emit("v", lambda: g.vector.memset(ap(out), c), [out], [])
 
     def act(out, i, f, scale=1.0):
-        emit("s", lambda: g.scalar.activation(ap(out), ap(i), f, scale=scale), [out], [i])
+        emit("s", lambda: g.scalar.activation(ap(out), ap(i), f, scale=ap(scale)), [out], [i, scale])
 
     def mm(out, l, r, start=True, stop=True):
         emit("t", lambda: g.tensor.matmul(ap(out), ap(l), ap(r), start, stop), [out], [l, r])
@@ -168,12 +168,15 @@ def rank_program(g, core, T, topo):
         fin.append(dmas("y" if n != "act" else "s", [(A(n, 0, w), None, T[n][:, 0:w], src[:, 0:w])]))
 
     ms(A("ones"), 1.0)
-    ms(A("us"), 1.0)
+    ms(A("rl"), 1.0)
     iota(F("i16"), [[1, 16]], 0, 0)
     iota(F("pi", 1), [[0, 1]], 0, 1)
-    asel(A("bw"), A("us"), [[1, 16], [0, 8], [-1, 16]], O.is_equal, 0, 0)
-    asel(A("bw"), A("bw"), [[0, 16], [-16, 8], [0, 16]], O.is_ge, 0, 1)
-    asel(A("bw"), A("bw"), [[0, 16], [16, 8], [0, 16]], O.is_ge, 15, -1)
+    cp1 = A("el", 0, 1024)
+    iota(cp1, [[1, 1024]], 1, 0)
+    iota(F("l16"), [[16, 16]], 0, 0)
+    iota(F("c64", 64), [[16, 64]], 0, 0)
+    m8 = A("tg", 384, 512)
+    iota(m8, [[1, 128]], 0, 0)
     wb = {}
 
     def W1(name, buf="wb"):
@@ -188,15 +191,13 @@ def rank_program(g, core, T, topo):
     asel(BB, o128, [[-16, 8], [0, 16]], O.is_ge, 0, 1)
     asel(BB, BB, [[16, 8], [0, 16]], O.is_ge, 15, -1)
     asel(ID, o128, [[-1, 128]], O.is_equal, 0, 1)
+    asel(A("bw"), A("rl"), [[1, 16], [0, 8], [-1, 16]], O.is_equal, 0, 0)
+    asel(A("bw"), A("bw"), [[0, 16], [-16, 8], [0, 16]], O.is_ge, 0, 1)
+    asel(A("bw"), A("bw"), [[0, 16], [16, 8], [0, 16]], O.is_ge, 15, -1)
     asel(SP, o128, [[-1, 128]], O.is_equal, 16, 1)
     asel(SN, o128, [[-1, 128]], O.is_equal, -16, 1)
     asel(TW, BB, [[1, 128]], O.is_gt, 0, -1)
-    cp1 = A("el", 0, 1024)
-    iota(cp1, [[1, 1024]], 1, 0)
-    iota(F("l16"), [[16, 16]], 0, 0)
-    iota(F("c64", 64), [[16, 64]], 0, 0)
-    m8 = A("tg", 384, 512)
-    iota(m8, [[1, 128]], 0, 0)
+    iota(A("rb"), [[1, 2048]], 0, 0)
     pi = S("si", "pi", 1)
     kcol, mO, mE = F("kcol", 1), F("mO", 1), F("mE", 1)
     cp(pi, F("pi", 1))
@@ -237,7 +238,34 @@ def rank_program(g, core, T, topo):
         ts(ck1, ci, F("k11", 1), O.is_equal)
         ts(ck0, ck0, RM(8), O.mult)
         tt(A("ck16", 512 * h, 512 * h + 512), ck0, ck1, O.add)
-    ts(A("d0"), A("us", 0, 1024), RM(2), O.mult)
+    ts(A("d0"), A("rl", 0, 1024), RM(2), O.mult)
+
+    def mk(name, src, col, w=1.0, buf="wm"):
+        m = W1(name, buf)
+        ts(m, src, col, O.mult, float(w), O.mult)
+        return m
+
+    one = F("one1", 1)
+    ms(one, 1.0)
+    I16 = mk("I16", ID, one)
+    mi = S("si", "mi", 128)
+    par, ta, tb = A("tg", 256, 384), A("tg", 0, 128), A("tg", 128, 256)
+    cp(mi, m8)
+    ts(mi, mi, 15, O.bitwise_and)
+    ts(ta, mi, 2.0, O.is_equal)
+    for r in (3.0, 7.0):
+        ts(tb, mi, r, O.is_equal)
+        tt(ta, ta, tb, O.add)
+    BB237 = W1("BB237", "wb")
+    tt(BB237, BB, ta, O.mult)
+    ts(A("us", 0, 1024), A("mlt"), 2048.0, O.is_lt)
+    for k in range(2):
+        mms(A("psB", 512 * k, 512 * k + 512), [(BB237, A("us", 512 * k, 512 * k + 512)), (I16, A("ck16", 512 * k, 512 * k + 512))])
+    cp(A("sz", 0, 1024), A("psB", 0, 1024))
+    scan(A("bt", 0, 1024), A("d0"), A("sz", 0, 1024), O.mult, O.add)
+    cp(A("bt16"), A("bt", 0, 1024))
+    cp(A("lt16"), A("bt", 0, 1024, 4))
+    ms(A("ks", 0, 2048), 0.0)
     names = ["E", "n", "r8", "cid", "P", "np", "st"]
     terms = [[(2, 1), (3, -1), (6, 1), (7, 1)], [(7, 1)], [(8, 1)], [(1, 1)], [(0, 16), (10, 1)], [(2, 1), (3, -1), (5, 1)], [(2, 1), (3, -1), (6, 1)]]
     ccol = {}
@@ -247,10 +275,12 @@ def rank_program(g, core, T, topo):
         return lambda w: A("sets", 2048 * i + 128 * w, 2048 * i + 128 * w + 128)
     for i, nm in enumerate(names):
         ccol[nm] = coef(nm, terms[i])
-        ts(A("sets", 2048 * i, 2048 * i + 2048), A("bw"), ccol[nm], O.mult)
+    for nm in ("np", "n", "cid", "P", "E", "r8", "st"):
+        i = names.index(nm)
+        act(A("sets", 2048 * i, 2048 * i + 2048), A("bw"), AF.Copy, ccol[nm])
     wf = F("wf", 1)
     cp(wf, A("wtc"))
-    ts(A("wts"), A("bw"), wf, O.mult)
+    act(A("wts"), A("bw"), AF.Copy, wf)
 
     def bws(w):
         return A("bw", 128 * w, 128 * w + 128)
@@ -265,14 +295,6 @@ def rank_program(g, core, T, topo):
     for w in range(16):
         ts(ors(w), BB, RM(w), O.mult)
 
-    def mk(name, src, col, w=1.0, buf="wm"):
-        m = W1(name, buf)
-        ts(m, src, col, O.mult, float(w), O.mult)
-        return m
-
-    one = F("one1", 1)
-    ms(one, 1.0)
-    I16 = mk("I16", ID, one)
     PE_, PO_, P01, P10 = mk("PE", ID, mE), mk("PO", ID, mO), mk("P01", SP, mE), mk("P10", SN, mO)
     BBK, BBS, BBN = mk("BBK", BB, one, 2048.0, "wb"), mk("BBS", BB, one, -8.0, "wb"), mk("BBN", BB, one, -1.0, "wb")
     RKS, RKB = mk("RKS", BB, RM(0), -0.5), mk("RKB", BB, RM(0), -128.0)
@@ -280,14 +302,10 @@ def rank_program(g, core, T, topo):
     RPS = mk("RPS", BB, coef("ks", [(0, 2.0 ** -8), (10, 2.0 ** -12), (9, 2048)]))
     CDP, CDN = mk("CDP", BB, RM(1)), mk("CDN", BB, RM(1), -1.0)
     STR, NRP = mk("STR", BB, ccol["st"]), mk("NRP", BB, ccol["n"])
-    CLS = [mk("CLS%d" % m, BB, RM(11 + m), 64.0) for m in range(4)]
-    mi = S("si", "mi", 128)
-    cp(mi, m8)
+    CLS = [mk("CLS%d" % m, BB, RM(11 + m), 64.0, "wb") for m in range(4)]
     ts(mi, mi, 1, O.bitwise_and)
-    par = A("tg", 256, 384)
     cp(par, mi)
     RPB = W1("RPB", "wm")
-    ta, tb = A("tg", 0, 128), A("tg", 128, 256)
     ts(ta, BB, coef("kb1", [(10, 1.0), (0, -1.0)]), O.mult)
     tt(ta, ta, par, O.mult)
     ts(tb, BB, coef("kb2", [(0, 1.0), (9, 2048.0)]), O.mult)
@@ -312,9 +330,6 @@ def rank_program(g, core, T, topo):
     RPP = mk("RPP", BB, ccol["P"])
     H0, PX10, H10, C1 = rowmap("H0", 0, [0]), W1("PX10", "wm"), rowmap("H10", 0, [10], -16), rowmap("C1", 0, [1])
     cp(PX10, bws(10))
-    BB237 = W1("BB237", "wb")
-    tt(ta, bws(2), bws(3), O.add)
-    tt(BB237, ta, bws(7), O.add)
     ms(A("mr"), 1.0)
     ms(A("mr", 0, 1536, 16), 0.0)
     ms(A("mrb"), 0.0)
@@ -323,7 +338,6 @@ def rank_program(g, core, T, topo):
         ms(A(n), 0.0)
     ms(A("vs"), 0.0)
     ms(A("zd"), 0.0)
-    ms(A("gt", 0, 2048), 0.0)
     ms(F("neg"), -1.0)
     cp(A("r16", 0, 16), F("neg"))
     lims = F("lims", 2)
@@ -378,36 +392,141 @@ def rank_program(g, core, T, topo):
         for k in range(4):
             act(A("r16", 16 + 512 * k, 528 + 512 * k), A(R, 512 * k, 512 * k + 512), AF.Copy)
         gathO("r16", 16, 2048, setof("P"), sub(B1, 0, 128))
-        gathO("r16", 16, 2048, setof("cid"), sub(B2_, 0, 128))
         cp(PO, sub(B1, 0, 128))
+        gather_xs()
+        for k in range(4):
+            c = (B0, B3)[k % 2]
+            mms(c, [(CDP, A("r16", 16 + 512 * k, 528 + 512 * k)), (CDN, A("r16", 15 + 512 * k, 527 + 512 * k))])
+            ts(A("m0", 512 * k, 512 * k + 512), c, 0.0, O.is_equal)
+        gathO("r16", 16, 2048, setof("cid"), sub(B2_, 0, 128))
         cp(CQF, sub(B2_, 0, 128))
         cp(CQ, CQF)
-        for k in range(4):
-            mms(A("psA", 512 * k, 512 * k + 512), [(CDP, A("r16", 16 + 512 * k, 528 + 512 * k)), (CDN, A("r16", 15 + 512 * k, 527 + 512 * k))])
-            ts(A("m0", 512 * k, 512 * k + 512), A("psA", 512 * k, 512 * k + 512), 0.0, O.is_equal)
         scan(A("rk"), A("m0"), A("m0"), O.mult, O.add)
 
     def gather_xs():
-        for k in range(4):
+        cp(A("xs", 1024, 2048), X(A("xa", 0, 2048), chunks(PO, 1, 2)))
+        for k in range(2):
             act(A("xs", 512 * k, 512 * k + 512), X(A("xa", 0, 2048), chunks(PO, k, 4)), AF.Copy)
 
-    def agents(POx):
-        cp(X(A("at"), POx), A("gt", 0, 2048))
+    POS = S("su", "pos", 128)
+
+    def agents():
+        for k in range(4):
+            act(A("at", 512 * k, 512 * k + 512), X(A("gt", 0, 2048), chunks(POS, k, 4)), AF.Copy)
 
     def build_xc(m):
-        act(A("g16"), A("at"), AF.Copy)
+        act(A("rl"), A("at"), AF.Copy)
         for k in range(4):
-            c = A("psA", 512 * k, 512 * k + 512)
-            mms(c, [(ID, A("xa", 512 * k, 512 * k + 512)), (CLS[m], A("g16", 512 * k, 512 * k + 512))])
+            c = (B0, B3)[k % 2]
+            mms(c, [(ID, A("xa", 512 * k, 512 * k + 512)), (CLS[m], A("rl", 512 * k, 512 * k + 512))])
             act(A("xc", 512 * k, 512 * k + 512), c, AF.Copy)
 
-    ts(A("us", 0, 1024), A("mlt"), 2048.0, O.is_lt)
-    for k in range(2):
-        mms(A("psB", 512 * k, 512 * k + 512), [(BB237, A("us", 512 * k, 512 * k + 512)), (I16, A("ck16", 512 * k, 512 * k + 512))])
-    cp(A("sz", 0, 1024), A("psB", 0, 1024))
-    scan(A("bt", 0, 1024), A("d0"), A("sz", 0, 1024), O.mult, O.add)
-    cp(A("bt16"), A("bt", 0, 1024))
-    cp(A("lt16"), A("bt", 0, 1024, 4))
+    def new_pos():
+        for k in range(4):
+            act(A("gt", 512 * k, 512 * k + 512), X(A("ks", 2080, 4128), chunks(POS, k, 4)), AF.Copy)
+            act(A("g16", 512 * k, 512 * k + 512), A("gt", 512 * k, 512 * k + 512), AF.Copy)
+        gathO("g16", 0, 2048, s0s, sub(B2_, 0, 128))
+
+    def s_keys():
+        for k in range(4):
+            mm(A("psA", 512 * k, 512 * k + 512), RKS, A("rk", 512 * k, 512 * k + 512), True, False)
+            mm(A("psA", 512 * k, 512 * k + 512), RPS, A("r16", 16 + 512 * k, 528 + 512 * k), False, False)
+        for k in range(4):
+            mm(A("psA", 512 * k, 512 * k + 512), BBS, A("xs", 512 * k, 512 * k + 512), False, True)
+
+    def u_scan():
+        scan(A("us"), A("m0"), A("xs", 0, 2048), O.mult, O.max)
+
+    def k_scan():
+        scan(A("ks", 0, 2048), A("m0"), A("psA"), O.mult, O.max)
+
+    def empties():
+        act(A("bt16"), A("sz", 0, 1024), AF.Copy)
+        gathO("bt16", 0, 1024, setof("n"), sub(B2_, 0, 64))
+        e64, r64 = F("e64", 64), F("r64", 64)
+        ts(e64, sub(B2_, 0, 64), 0.5, O.is_lt)
+        cp(S("sb", "e64", 64), e64)
+        e = prefix(S("sb", "e64", 64), 64, r64, "pe", sub(B2_, 64, 192))
+        cp(F("ecnt", 1), e)
+        ts(F("t64", 64), c4, 256.0, O.add)
+        ts(F("u64", 64), r64, 255.5, O.is_lt)
+        tt(e64, e64, F("u64", 64), O.mult)
+        choose(r64, e64, r64, F("t64", 64), "ch64", 64)
+        cp(S("su", "l64", 64), r64)
+        cp(X(A("el"), S("su", "l64", 64)), A("ck16"))
+
+    def send(dst, out, src, rs, ls):
+        rid, pid, _ = topo.addr(dst)
+        es = topo.engines(core, dst)[:4]
+        m = 0
+        for e in es:
+            m |= 1 << e
+        SEM[ls] = ls
+        touch("g", [], [src], (ls, len(es)))
+        g.remote_dma(out_ap=T[out][:], in_ap=ap(src), remote_sem=T.sem[rs], local_sem=T.sem[ls], pid=pid, routing_id=rid, dma_engine_mask=m)
+        fin.append((ls, len(es)))
+
+    def arrived(buf, rs, src):
+        n = len(topo.engines(src, core)[:4])
+        SEM[rs] = rs
+        hist[(rs, n)] = {}
+        recs.setdefault(buf, []).append([0, 96, rs, n, True])
+        fin.append((rs, n))
+
+    def visits(t, q, h):
+        IN = "in%d" % t
+        arrived(IN, "ra%d" % t, h)
+        for w in range(16):
+            mm(sub(B3, 0, 6), wtw(w), A(IN, w, 96, 16), w == 0, w == 15)
+        vi = S("si", "vi", 6)
+        cp(vi, sub(B3, 0, 6))
+        ts(vi, vi, 2047, O.bitwise_and)
+        cp(S("su", "vi", 6), vi)
+        cp(A("vag"), X(A("at"), S("su", "vi", 6)))
+        mm(sub(B3, 16, 112), STR, A("vag"))
+        mm(sub(B3, 112, 208), NRP, A("vag"))
+        cp(A("zb", 0, 1536, 16), A(IN))
+        scan(A("xr", 0, 1536), A("mr", 0, 1536), A("zb", 0, 1536), O.mult, O.add)
+        yield
+        hl = F("hl", 96)
+        ts(hl, sub(B3, 112, 208), -1.0, O.add, kcol, O.min)
+        tt(hl, hl, sub(B3, 16, 112), O.add)
+        cp(S("su", "hl", 96), hl)
+        hx = A("sqs", 0, 1536)
+        tt(hx, X(A("xs", 0, 2048), S("su", "hl", 96)), A("xr", 0, 1536), O.subtract)
+        act(hx, hx, AF.Square)
+        for w in range(16):
+            mm(sub(B3, 208, 214), setof("st")(w), A("vag", w, 96, 16), w == 0, w == 15)
+        for i in range(16):
+            mm(sub(B0, 256, 352), bws(i), A("sqs", i, 1536, 16), i == 0, i == 15)
+        yield
+        ts(A("tg", 0, 96), sub(B0, 256, 352), 16.0, O.mult, kcol, O.add)
+        vtr(A("tt", 0, 96), A("tg", 0, 96))
+        scan(A("tg", 0, 96), A("mrb", 0, 96), A("tt", 0, 96), O.max, O.min)
+        k6 = S("si", "k6", 6)
+        cp(k6, A("tg", 15, 96, 16))
+        ts(k6, k6, 15, O.bitwise_and)
+        cp(S("sh", "k6", 6), k6)
+        s2o(S("sh", "k6", 6), sub(B3, 224, 230), 6)
+        yield
+        y6 = F("y6", 6)
+        cp(y6, sub(B3, 224, 230))
+        tt(y6, y6, sub(B3, 208, 214), O.add)
+        cp(S("su", "y6", 6), y6)
+        cp(A("yv"), X(A("xs", 0, 2048), S("su", "y6", 6)))
+        send(h, "ry%d" % t, A("yv"), "rb%d" % t, "lb%d" % t)
+        yield
+        arrived("ry%d" % t, "rb%d" % t, q)
+        tt(A("ri"), A("ry%d" % t), A("vs", 0, 96), O.add)
+        ts(A("ri"), A("ri"), 1, O.arith_shift_right)
+        cp(A("res", 0, 96), A("ri"))
+        cp(A("nx"), X(A("res"), S("su", "vL")))
+        cp(X(A("xa"), S("su", "vA")), A("nx"))
+        if t < 3:
+            cp(X(A("xs"), S("su", "vP")), A("nx"))
+            cp(X(A("xc"), S("su", "vA")), A("nx"))
+        yield
+
     gathO("bt16", 0, 1024, setof("np"), sub(B2_, 0, 64))
     gathO("bt16", 0, 1024, setof("n"), sub(B2_, 64, 128))
     t64, u64 = F("t64", 64), F("u64", 64)
@@ -417,13 +536,13 @@ def rank_program(g, core, T, topo):
     cp(s64, sub(B2_, 0, 64))
     choose(s64, u64, s64, t64, "ch64", 64)
     cp(S("su", "l64", 64), s64)
-    cp(X(A("gt"), S("su", "l64", 64)), cp1)
-    ts(A("m0"), A("gt", 0, 2048), 0.0, O.is_equal)
-    scan(A("ks", 0, 2048), A("m0"), A("gt", 0, 2048), O.mult, O.add)
-    ts(A("g16"), A("ks", 0, 2048), -1.0, O.add)
+    cp(X(A("ks", 0, 3072), S("su", "l64", 64)), cp1)
+    ts(A("m0"), A("ks", 0, 2048), 0.0, O.is_equal)
+    scan(A("g16"), A("m0"), A("ks", 0, 2048), O.mult, O.add)
     ms(A("el"), 0.0)
+    r91 = coef("r91", [(9, 1), (1, -1)])
     gathO("g16", 0, 2048, s0s, sub(B2_, 0, 128))
-    cp(CQF, sub(B2_, 0, 128))
+    ts(CQF, sub(B2_, 0, 128), -1.0, O.add)
     cp(CQ, CQF)
     scan(A("rk"), A("m0"), A("m0"), O.mult, O.add)
     ts(A("rl"), A("rk"), kcol, O.is_equal)
@@ -435,17 +554,24 @@ def rank_program(g, core, T, topo):
         ts(A("ai"), A("psA", *c), 0.0625, O.mult, -0.46875, O.add)
         cp(A("bt16", 0, 512), A("ai"))
         mms(A("psB", *c), [(H0, A("bt16", 0, 512)), (PX10, px), (H10, A("bt16", 0, 512)), (C1, A("g16", *c))])
-        ts(A("ra", *c), A("psB", *c), RM(9), O.add)
+        ts(A("ra", *c), A("psB", *c), r91, O.add)
     for k in range(4):
         act(A("r16", 16 + 512 * k, 528 + 512 * k), A("ra", 512 * k, 512 * k + 512), AF.Copy)
     gathO("r16", 16, 2048, setof("P"), sub(B1, 0, 128))
     cp(PO, sub(B1, 0, 128))
+    gather_xs()
+    cp(X(A("at"), PO), A("rb"))
     for k in range(4):
         act(A("gt", 512 * k, 512 * k + 512), X(A("bt", 0, 1024), chunks(CQ, k, 4)), AF.Copy)
-    agents(PO)
-    gather_xs()
-    build_xc(0)
+    act(A("g16"), A("at"), AF.Copy)
+    empties()
+    gathO("g16", 0, 2048, s0s, sub(B2_, 256, 384))
     R = ["ra", "rb"]
+    gens = []
+
+    def vstep():
+        if gens:
+            next(gens[0])
 
     for t in range(4):
         cl = t
@@ -457,11 +583,13 @@ def rank_program(g, core, T, topo):
         for o in (EU, sub(ED2, 0, 32, 2), sub(ED2, 1, 32, 2)):
             ts(o, sub(B1, 0, 16), -1.0, O.add)
         cp(nc, sub(B1, 16, 32))
-        scan(A("us"), A("m0"), A("xs", 0, 2048), O.mult, O.max)
-        for k in range(4):
-            c = (512 * k, 512 * k + 512)
-            mms(A("psA", *c), [(RKS, A("rk", *c)), (RPS, A("r16", 16 + 512 * k, 528 + 512 * k)), (BBS, A("xs", *c))])
-        scan(A("ks", 0, 2048), A("m0"), A("psA"), O.mult, O.max)
+        s_keys()
+        u_scan()
+        cp(A("uc"), X(A("us"), EU))
+        k_scan()
+        vstep()
+        for w in range(16):
+            mm(sub(B1, 32, 48), bws(w), A("uc", w, 256, 16), w == 0, w == 15)
         lanes_of(A("ks", 0, 2048), ED2)
         sel(F("key"), 0, F("mE4", 1), F("mO4", 1))
         ki, k2 = S("si", "ki"), S("si", "k2")
@@ -474,6 +602,52 @@ def rank_program(g, core, T, topo):
         cp(S("su", "hU"), k2)
         cp(A("acq"), X(A("act"), S("su", "hU")))
         cp(A("xsb"), X(A("xa", 0, 2048), S("su", "sU")))
+        cp(A("xl", *lanes), A("xsb"))
+        for k in range(4):
+            c = (512 * k, 512 * k + 512)
+            mm(A("psA", *c), RKB, A("rk", *c), True, False)
+            mm(A("psA", *c), RPB, A("r16", 16 + 512 * k, 528 + 512 * k), False, False)
+            tt(A("df", *c), X(A("xl"), chunks(CQ, k, 4)), A("xs", *c), O.subtract)
+            act(A("sqs", *c), A("df", *c), AF.Square)
+        vstep()
+        for k in range(4):
+            mm(A("psA", 512 * k, 512 * k + 512), BBK, A("sqs", 512 * k, 512 * k + 512), False, True)
+        ts(k2, ki, 11, O.arith_shift_right)
+        ts(F("y"), k2, -1.0, O.mult, 4096.0, O.add)
+        cp(ki, F("y"))
+        ts(k2, ki, 4, O.arith_shift_right)
+        cp(sig, k2)
+        ts(k2, ki, 15, O.bitwise_and)
+        cp(rnk, k2)
+        vstep()
+        if t == 0:
+            cp(POS, sub(B2_, 256, 384))
+            agents()
+        build_xc(cl)
+        gr, live, want0 = F("gr"), F("live"), F("want0")
+        tt(gr, sub(B1, 32, 48), sig, O.subtract)
+        ts(live, nc, 0.5, O.is_gt)
+        ts(want0, gr, sub(lims, 1, 2), O.is_gt)
+        tt(want0, want0, live, O.mult)
+        ai0, ai1 = A("ai", 0, 256), A("ai", 256, 512)
+        cp(ai0, A("acq"))
+        ts(ai1, ai0, 15, O.bitwise_and)
+        ts(ai0, ai0, 4, O.arith_shift_right)
+        ts(A("ahl"), A("ai"), F("k128", 1), O.add, 1.0 / 2048, O.mult)
+        scan(A("gt", 0, 2048), A("m0"), A("psA"), O.mult, O.max)
+        lanes_of(A("gt", 0, 2048), ED2)
+        sel(F("kb0"), 0)
+        sel(F("kb1"), 1)
+        cp(ki, F("kb0"))
+        ts(ki, ki, 127, O.bitwise_and)
+        cp(k2, F("kb1"))
+        ts(k2, k2, 15, O.bitwise_and)
+        bf = F("bf")
+        ts(bf, ki, 16.0, O.mult)
+        tt(bf, bf, k2, O.add)
+        vstep()
+        if t:
+            s_keys()
         for k in range(4):
             z0 = 1024 * (k % 2)
             c = (z0, z0 + 1024)
@@ -483,45 +657,8 @@ def rank_program(g, core, T, topo):
             act(A("df", *c), A("df", *c), AF.Square)
             for i in range(16):
                 mm(A("psB", 64 * k, 64 * k + 64), bws(i), A("df", z0 + i, z0 + 1024, 16), i == 0, i == 15)
-        cp(A("xl", *lanes), A("xsb"))
-        for k in range(4):
-            c = (512 * k, 512 * k + 512)
-            hc = A("hx", 512 * (k % 2), 512 * (k % 2) + 512)
-            tt(hc, X(A("xl"), chunks(CQ, k, 4)), A("xs", *c), O.subtract)
-            act(A("sqs", *c), hc, AF.Square)
-            mms(A("psA", *c), [(RKB, A("rk", *c)), (RPB, A("r16", 16 + 512 * k, 528 + 512 * k)), (BBK, A("sqs", *c))])
-        ts(k2, ki, 11, O.arith_shift_right)
-        ts(F("y"), k2, -1.0, O.mult, 4096.0, O.add)
-        cp(ki, F("y"))
-        ts(k2, ki, 4, O.arith_shift_right)
-        cp(sig, k2)
-        ts(k2, ki, 15, O.bitwise_and)
-        cp(rnk, k2)
-        cp(A("uc"), X(A("us"), EU))
-        for w in range(16):
-            mm(sub(B1, 32, 48), bws(w), A("uc", w, 256, 16), w == 0, w == 15)
-        gr, live, want0 = F("gr"), F("live"), F("want0")
-        tt(gr, sub(B1, 32, 48), sig, O.subtract)
-        ts(live, nc, 0.5, O.is_gt)
-        ts(want0, gr, sub(lims, 1, 2), O.is_gt)
-        tt(want0, want0, live, O.mult)
-        act(A("bt16"), A("sz", 0, 1024), AF.Copy)
-        gathO("bt16", 0, 1024, setof("n"), sub(B2_, 0, 64))
-        e64, r64 = F("e64", 64), F("r64", 64)
-        ts(e64, sub(B2_, 0, 64), 0.5, O.is_lt)
-        cp(S("sb", "e64", 64), e64)
-        ecnt = prefix(S("sb", "e64", 64), 64, r64, "pe", sub(B2_, 64, 192))
-        ts(F("t64", 64), c4, 256.0, O.add)
-        ts(F("u64", 64), r64, 255.5, O.is_lt)
-        tt(e64, e64, F("u64", 64), O.mult)
-        choose(r64, e64, r64, F("t64", 64), "ch64", 64)
-        cp(S("su", "l64", 64), r64)
-        cp(X(A("el"), S("su", "l64", 64)), A("ck16"))
-        ai0, ai1 = A("ai", 0, 256), A("ai", 256, 512)
-        cp(ai0, A("acq"))
-        ts(ai1, ai0, 15, O.bitwise_and)
-        ts(ai0, ai0, 4, O.arith_shift_right)
-        ts(A("ahl"), A("ai"), F("k128", 1), O.add, 1.0 / 2048, O.mult)
+        if t:
+            new_pos()
         for h in (0, 1):
             tt(A("tg", 256 * h, 256 * h + 256), sub(B0, 0, 256), A("ahl", 256 * h, 256 * h + 256), O.add)
         vtr(A("tt"), A("tg"))
@@ -542,23 +679,26 @@ def rank_program(g, core, T, topo):
         ts(S("su", "aU"), sub(B1, 48, 64), 2047.0, O.min)
         cp(A("ag16"), X(A("at"), S("su", "aU")))
         gathO("ag16", 0, 256, setof("E"), sub(B1, 64, 80))
-        gathO("ag16", 0, 256, setof("r8"), sub(B1, 80, 96))
-        gathO("ag16", 0, 256, setof("n"), sub(B1, 96, 112))
+        gathO("ag16", 0, 256, setof("r8"), sub(B3, 480, 496))
+        gathO("ag16", 0, 256, setof("n"), sub(B3, 496, 512))
+        if t:
+            u_scan()
+            k_scan()
         DU, DD2 = S("su", "du"), S("su", "dd2", 32)
         for o in (DU, sub(DD2, 0, 32, 2), sub(DD2, 1, 32, 2)):
             ts(o, sub(B1, 64, 80), -1.0, O.add)
         dn, df_, d47 = F("dn"), F("d"), F("d47")
-        cp(dn, sub(B1, 96, 112))
-        cp(df_, sub(B1, 80, 96))
+        cp(A("ud"), X(A("us"), DU))
+        cp(dn, sub(B3, 496, 512))
+        cp(df_, sub(B3, 480, 496))
         ts(d47, df_, -2047.0, O.add)
         tt(d47, d47, has, O.mult)
         ts(d47, d47, 2047.0, O.add)
         cp(S("sh", "d16"), d47)
         for w in range(16):
             mm(sub(B3, w, 256, 16), ors(w), S("sh", "d16"))
-        cp(A("drep"), sub(B3, 0, 256), "v")
-        cp(A("ud"), X(A("us"), DU))
         tt(A("uv"), A("uc"), A("ud"), O.max)
+        cp(A("drep"), sub(B3, 0, 256))
         for w in range(16):
             mm(sub(B1, 112, 128), bws(w), A("uv", w, 256, 16), w == 0, w == 15)
         for u in range(16):
@@ -579,6 +719,8 @@ def rank_program(g, core, T, topo):
         cp(ki, F("y"))
         ts(k2, ki, 4, O.arith_shift_right)
         cp(F("sigd"), k2)
+        if t:
+            cp(POS, sub(B2_, 0, 128))
         mer, tmp = F("mer"), F("tmp")
         tt(tmp, F("sigd"), sig, O.min)
         tt(tmp, sub(B1, 112, 128), tmp, O.subtract)
@@ -597,111 +739,96 @@ def rank_program(g, core, T, topo):
         tt(want, want0, tmp, O.mult)
         cp(S("sb", "wb"), want)
         prefix(S("sb", "wb"), 16, wk, "pw", sub(B1, 144, 176))
-        ts(tmp, wk, ecnt, O.is_lt)
+        ts(tmp, wk, F("ecnt", 1), O.is_lt)
         tt(spl, want, tmp, O.mult)
         cp(S("su", "kU"), wk)
         cp(A("eg16"), X(A("el"), S("su", "kU")))
-        scan(A("gt", 0, 2048), A("m0"), A("psA"), O.mult, O.max)
-        lanes_of(A("gt", 0, 2048), ED2)
-        sel(F("kb0"), 0)
-        sel(F("kb1"), 1)
-        cp(ki, F("kb0"))
-        ts(ki, ki, 127, O.bitwise_and)
-        cp(k2, F("kb1"))
-        ts(k2, k2, 15, O.bitwise_and)
-        bf = F("bf")
-        ts(bf, ki, 16.0, O.mult)
-        tt(bf, bf, k2, O.add)
         choose(bf, spl, bf, sf)
         cp(S("su", "bU"), bf)
         cp(A("xbb"), X(A("xa", 0, 2048), S("su", "bU")))
         cp(A("xb", *lanes), A("xbb"))
-        for k in range(4):
-            c = (512 * k, 512 * k + 512)
-            hc = A("hx", 512 * (k % 2), 512 * (k % 2) + 512)
-            tt(hc, X(A("xb"), chunks(CQ, k, 4)), A("xs", *c), O.subtract)
-            act(hc, hc, AF.Square)
-            mms(A("psA", *c), [(BB, hc), (BBN, A("sqs", *c))])
-            ts(A("g16", *c), A("psA", *c), 0.0, O.is_lt)
-        cp(A("xb", *lanes), A("xsb"))
-        scan(A("rl"), A("m0"), A("g16"), O.mult, O.add)
-        for src, o, st in (("g16", 0, s0s), ("rl", 128, bws), ("rk", 256, s0s)):
-            gathO(src, 0, 2048, st, sub(B2_, o, o + 128))
-        lanes_of(A("rl"), ED2)
-        nl = F("nl")
-        sel(nl, 0)
-        tt(nl, nl, spl, O.mult)
-        gathO("eg16", 0, 256, setof("r8"), sub(B1, 176, 192))
-        tl = F("tl")
-        ts(tl, lane, 1280.0, O.add)
-        choose(tmp, spl, sub(B1, 176, 192), tl)
-        cp(S("su", "eL"), tmp)
-        choose(tmp, mer, df_, tl)
-        cp(S("su", "dL"), tmp)
-        x1 = S("sh", "x1", 64)
+        x1, x2 = S("sh", "x1", 48), S("sh", "x2")
         tt(tmp, mer, dn, O.mult)
         tt(sub(x1, 0, 16), nc, tmp, O.add)
-        cp(sub(x1, 16, 32), nl)
-        cp(sub(x1, 32, 48), nc)
-        cp(sub(x1, 48, 64), df_)
+        cp(sub(x1, 16, 32), nc)
+        cp(sub(x1, 32, 48), df_)
         for w in range(16):
-            for h in (0, 1):
-                mm(A("psA", 512 * h + w, 512 * h + 512, 16), ors(w), sub(x1, 32 * h, 32 * h + 32))
-        act(A("x16"), A("psA", 0, 1024), AF.Copy)
-        xr_, xl_, xn_, xd_ = [A("x16", 256 * k, 256 * k + 256) for k in range(4)]
+            mm(A("psA", w, 512, 16), ors(w), sub(x1, 0, 32))
+            mm(A("psA", 512 + w, 768, 16), ors(w), sub(x1, 32, 48))
+        act(A("x16", 0, 768), A("psA", 0, 768), AF.Copy)
+        xr_, xn_, xd_, xl_ = [A("x16", 256 * k, 256 * k + 256) for k in range(4)]
         ckl = A("ck16", cl, 1024, 4)
-        p0, p1 = sub(B0, 0, 256), sub(B0, 256, 512)
-        mms(p0, [(M237, xr_), (M7N, xl_), (I16, ckl)])
-        mms(p1, [(M237, xl_), (I16, A("eg16"))])
+        p0, p1, p2 = sub(B0, 0, 256), sub(B0, 256, 512), sub(B3, 0, 256)
+        mms(p0, [(M237, xr_), (I16, ckl)])
+        gathO("eg16", 0, 256, setof("r8"), sub(B1, 176, 192))
+        gathO("rk", 0, 2048, s0s, sub(B1, 384, 512))
+        for k in range(4):
+            c = (512 * k, 512 * k + 512)
+            tt(A("df", *c), X(A("xb"), chunks(CQ, k, 4)), A("xs", *c), O.subtract)
+            act(A("df", *c), A("df", *c), AF.Square)
+            mms(A("psA", *c), [(BBN, A("sqs", *c)), (BB, A("df", *c))])
+        tl = F("tl")
+        ts(tl, lane, 1280.0, O.add)
+        choose(tmp, mer, df_, tl)
+        cp(S("su", "dL"), tmp)
         cp(A("sz", cl, 1024, 4), p0)
         cp(X(A("sz"), S("su", "dL")), A("zd"))
         scan(A("bt", 0, 1024), A("d0"), A("sz", 0, 1024), O.mult, O.add)
         cp(A("bl16"), A("bt", cl, 1024, 4))
-        cp(A("sze"), p1)
-        mms(p0, [(I16, A("bl16")), (M5, xn_), (M1N, xd_), (M81, ckl)])
-        mms(p1, [(I23, A("bl16")), (M56, xn_), (M567, xl_), (IX, A("eg16")), (M81N, ckl)])
-        gathO("bl16", 0, 256, setof("np"), sub(B1, 192, 208))
-        cp(A("dvt"), p0)
-        cp(A("bt", 1024, 1280), p1)
-        cp(A("lft"), p1)
-        p2 = sub(B3, 0, 256)
-        mms(p2, [(M237, xr_), (M237N, xl_), (I16, ckl)])
+        choose(tmp, spl, sub(B1, 176, 192), tl)
+        cp(S("su", "eL"), tmp)
+        for k in range(4):
+            c = (512 * k, 512 * k + 512)
+            ts(A("g16", *c), A("psA", *c), 0.0, O.is_lt)
+        cp(A("xb", *lanes), A("xsb"))
+        scan(A("rl"), A("m0"), A("g16"), O.mult, O.add)
+        gathO("g16", 0, 2048, s0s, sub(B2_, 0, 128))
+        lanes_of(A("rl"), ED2)
+        nl = F("nl")
+        sel(nl, 0)
+        tt(nl, nl, spl, O.mult)
+        cv, lv, cql, rp = F("cv", 128), F("lv", 128), F("cql", 128), F("rp", 128)
+        rkO, rlO = F("rkO", 128), F("rlO", 128)
+        cp(rkO, sub(B1, 384, 512))
+        cp(x2, nl)
+        for w in range(16):
+            mm(sub(p2, w, 256, 16), ors(w), x2)
+        cp(xl_, p2)
+        mms(p0, [(I16, A("bl16")), (M7N, xl_)])
+        mms(p1, [(I16, A("bl16")), (M5, xn_), (M1N, xd_), (M81, ckl), (M7N, xl_)])
+        mms(p2, [(I23, A("bl16")), (M56, xn_), (M567, xl_), (IX, A("eg16")), (M81N, ckl)])
+        gathO("rl", 0, 2048, bws, sub(B1, 256, 384))
+        cp(lv, sub(B2_, 0, 128))
+        ts(cv, CQF, -0.75, O.mult, 1024.0 - cl / 4.0, O.add)
+        tt(cv, cv, lv, O.mult)
+        tt(cql, cv, CQF, O.add)
+        cp(S("su", "cqL", 128), cql)
+        cp(A("bt", cl, 1024, 4), p0)
+        cp(A("bt", 1024, 1280), p2)
+        cp(A("lft"), p2)
+        cp(A("dvt"), p1)
         cp(X(A("bt"), S("su", "eL")), A("lft"))
         if t < 3:
             cp(A("lt16"), A("bt", cl + 1, 1024, 4))
         else:
             cp(A("bt16"), A("bt", 0, 1024))
         cp(X(A("bt"), S("su", "dL")), A("dvt"))
-        cp(A("sz", cl, 1024, 4), p2)
-        cp(X(A("sz"), S("su", "eL")), A("sze"))
-        stc = F("stc")
-        cp(stc, sub(B1, 192, 208))
-        cv, lv, cql, rp = F("cv", 128), F("lv", 128), F("cql", 128), F("rp", 128)
-        cp(lv, sub(B2_, 0, 128))
-        ts(cv, CQF, -0.75, O.mult, 1024.0 - cl / 4.0, O.add)
-        tt(cv, cv, lv, O.mult)
-        tt(cql, cv, CQF, O.add)
-        cp(S("su", "cqL", 128), cql)
         for k in range(4):
-            c = (512 * k, 512 * k + 512)
-            act(A("gt", *c), X(A("bt", 0, 1280), chunks(S("su", "cqL", 128), k, 4)), AF.Copy)
-            act(A("g16", *c), A("gt", *c), AF.Copy)
+            act(A("gt", 512 * k, 512 * k + 512), X(A("bt", 0, 1280), chunks(S("su", "cqL", 128), k, 4)), AF.Copy)
+        cp(A("g16"), X(A("bt", 0, 1280), S("su", "cqL", 128)))
         gathO("g16", 0, 2048, setof("np"), sub(B3, 256, 384))
-        rkO, rlO = F("rkO", 128), F("rlO", 128)
-        cp(rkO, sub(B2_, 256, 384))
-        ts(rlO, sub(B2_, 128, 256), 0.0625, O.mult)
+        mms(p0, [(M237, xr_), (M237N, xl_), (I16, ckl)])
+        mms(p1, [(M237, xl_), (I16, A("eg16"))])
+        gathO("bl16", 0, 256, setof("np"), sub(B2_, 192, 208))
+        agents()
+        ts(rlO, sub(B1, 256, 384), 0.0625, O.mult)
         tt(rp, rkO, rlO, O.subtract)
         tt(rlO, rlO, rp, O.subtract)
         ts(rlO, rlO, -1.0, O.add)
         tt(rlO, rlO, lv, O.mult)
         tt(rp, rp, rlO, O.add)
-        tt(rp, rp, sub(B3, 256, 384), O.add)
-        cp(S("su", "npL", 128), rp)
-        tt(X(A(R[1]), S("su", "npL", 128)), A("gt", 0, 2048), A(R[0]), O.add)
-        R = R[::-1]
-        agents(PO)
-        order_tables(R[0])
-        gather_xs()
+        stc = F("stc")
+        cp(stc, sub(B2_, 192, 208))
         idle, visit, vk = F("idle"), F("visit"), F("vk")
         tt(tmp, mer, spl, O.add)
         tt(idle, live, tmp, O.subtract)
@@ -722,25 +849,26 @@ def rank_program(g, core, T, topo):
         q = T.cores[(rank + 1 + t % 7) % 8]
         h = T.cores[(rank - 1 - t % 7) % 8]
 
-        def send(dst, out, src, rs, ls):
-            rid, pid, _ = topo.addr(dst)
-            es = topo.engines(core, dst)[:4]
-            m = 0
-            for e in es:
-                m |= 1 << e
-            SEM[ls] = ls
-            touch("g", [], [src], (ls, len(es)))
-            g.remote_dma(out_ap=T[out][:], in_ap=ap(src), remote_sem=T.sem[rs], local_sem=T.sem[ls], pid=pid, routing_id=rid, dma_engine_mask=m)
-            fin.append((ls, len(es)))
-
-        def arrived(buf, rs, src):
-            n = len(topo.engines(src, core)[:4])
-            SEM[rs] = rs
-            hist[(rs, n)] = {}
-            recs.setdefault(buf, []).append([0, 96, rs, n, True])
-            fin.append((rs, n))
-
         send(q, "in%d" % t, A("vs", 0, 96), "ra%d" % t, "la%d" % t)
+        cp(A("res", 96, 352), A("xsb"))
+        tt(rp, rp, sub(B3, 256, 384), O.add)
+        cp(S("su", "npL", 128), rp)
+        if t < 3:
+            cp(S("sh", "rp16", 128), rp)
+            for w in range(16):
+                for k in range(4):
+                    mm(A("psA", 512 * k + w, 512 * k + 512, 16), ors(w), chunks(S("sh", "rp16", 128), k, 4))
+            act(A("ks", 2080, 4128), A("psA"), AF.Copy)
+        tt(X(A(R[1]), S("su", "npL", 128)), A("gt", 0, 2048), A(R[0]), O.add)
+        R = R[::-1]
+        cp(A("sz", cl, 1024, 4), p0)
+        cp(A("sze"), p1)
+        cp(X(A("sz"), S("su", "eL")), A("sze"))
+        if t < 3:
+            empties()
+        order_tables(R[0])
+        gens[:] = [visits(t, q, h)]
+        vstep()
         if t < 3:
             mt = S("sb", "mt")
             cp(mt, mer)
@@ -750,55 +878,6 @@ def rank_program(g, core, T, topo):
             cp(zi, F("zz", 1))
             ts(zi, zi, 15, O.bitwise_and)
             tt(limz, sub(lims, 0, 1), zi, O.add)
-            build_xc(cl + 1)
-        arrived("in%d" % t, "ra%d" % t, h)
-        IN = "in%d" % t
-        for w in range(16):
-            mm(sub(B1, 256, 262), wtw(w), A(IN, w, 96, 16), w == 0, w == 15)
-        vi = S("si", "vi", 6)
-        cp(vi, sub(B1, 256, 262))
-        ts(vi, vi, 2047, O.bitwise_and)
-        cp(S("su", "vi", 6), vi)
-        cp(A("vag"), X(A("at"), S("su", "vi", 6)))
-        mm(sub(B1, 272, 368), STR, A("vag"))
-        mm(sub(B1, 368, 464), NRP, A("vag"))
-        hl = F("hl", 96)
-        ts(hl, sub(B1, 368, 464), -1.0, O.add, kcol, O.min)
-        tt(hl, hl, sub(B1, 272, 368), O.add)
-        cp(S("su", "hl", 96), hl)
-        cp(A("zb", 0, 1536, 16), A(IN))
-        scan(A("xr", 0, 1536), A("mr", 0, 1536), A("zb", 0, 1536), O.mult, O.add)
-        tt(A("hx"), X(A("xs", 0, 2048), S("su", "hl", 96)), A("xr", 0, 1536), O.subtract)
-        act(A("hx"), A("hx"), AF.Square)
-        for i in range(16):
-            mm(sub(B0, 0, 96), bws(i), A("hx", i, 1536, 16), i == 0, i == 15)
-        ts(A("tg", 0, 96), sub(B0, 0, 96), 16.0, O.mult, kcol, O.add)
-        vtr(A("tt", 0, 96), A("tg", 0, 96))
-        scan(A("tg", 0, 96), A("mrb", 0, 96), A("tt", 0, 96), O.max, O.min)
-        k6 = S("si", "k6", 6)
-        cp(k6, A("tg", 15, 96, 16))
-        ts(k6, k6, 15, O.bitwise_and)
-        cp(S("sh", "k6", 6), k6)
-        s2o(S("sh", "k6", 6), sub(B1, 464, 470), 6)
-        for w in range(16):
-            mm(sub(B2_, 384, 390), setof("st")(w), A("vag", w, 96, 16), w == 0, w == 15)
-        y6 = F("y6", 6)
-        cp(y6, sub(B1, 464, 470))
-        tt(y6, y6, sub(B2_, 384, 390), O.add)
-        cp(S("su", "y6", 6), y6)
-        cp(A("yv"), X(A("xs", 0, 2048), S("su", "y6", 6)))
-        send(h, "ry%d" % t, A("yv"), "rb%d" % t, "lb%d" % t)
-        arrived("ry%d" % t, "rb%d" % t, q)
-        tt(A("ri"), A("ry%d" % t), A("vs", 0, 96), O.add)
-        ts(A("ri"), A("ri"), 1, O.arith_shift_right)
-        cp(A("res", 0, 96), A("ri"))
-        cp(A("res", 96, 352), A("xsb"))
-        cp(A("nx"), X(A("res"), S("su", "vL")))
-        cp(X(A("xa"), S("su", "vA")), A("nx"))
-        if t < 3:
-            cp(X(A("xc"), S("su", "vA")), A("nx"))
-            cp(X(A("xs"), S("su", "vP")), A("nx"))
-    fin.append(dmas("y", [(None, A("xa", 0, 2048), T.yx[:, 0:2048], T["xa"][:, 0:2048])]))
     for k in range(4):
         mm(A("psA", 512 * k, 512 * k + 512), RPP, A("r16", 16 + 512 * k, 528 + 512 * k))
         act(A("ks", 512 * k, 512 * k + 512), A("psA", 512 * k, 512 * k + 512), AF.Copy)
@@ -806,14 +885,19 @@ def rank_program(g, core, T, topo):
     fin.append(dmas("y", [(A("gt", 0, 2048), A("ks"), T["gt"][k::16, 0:2048], T["ks"][k::16, k:k + 2048]) for k in range(16)]))
     gathO("bt16", 0, 1024, setof("st"), sub(B2_, 0, 64))
     ts(S("su", "l64", 64), sub(B2_, 0, 64), 2047.0, O.min)
+    vstep()
     for k in range(2):
-        mm(A("psB", 512 * k, 512 * k + 512), NRP, A("bt16", 512 * k, 512 * k + 512))
+        mm(A("psA", 512 * k, 512 * k + 512), NRP, A("bt16", 512 * k, 512 * k + 512))
     ye, yb = A("el", 0, 1024), A("bt", 0, 1024)
-    ts(yb, A("psB", 0, 1024), kcol, O.is_gt)
+    ts(yb, A("psA", 0, 1024), kcol, O.is_gt)
+    vstep()
+    vstep()
     cp(ye, X(A("gt", 0, 2048), S("su", "l64", 64)))
     ts(ye, ye, -2048.0, O.add)
     tt(ye, ye, yb, O.mult)
     ts(ye, ye, 2048.0, O.add)
     fin.append(dmas("y", [(None, ye, T.ym[:, 0:1024], T["el"][:, 0:1024])]))
+    vstep()
+    fin.append(dmas("y", [(None, A("xa", 0, 2048), T.yx[:, 0:2048], T["xa"][:, 0:2048])]))
     for who, v in fin + [(e, cnt[e]) for e in ("v", "s", "t", "g")]:
         g.wait_ge(T.sem[SEM[who]], v)

@@ -388,14 +388,16 @@ def rank_program(g, core, T, topo):
         w = (off[2] - off[1]) // n
         return sub(off, k * w, k * w + w)
 
-    def order_tables(R):
+    def order_tables(R, last):
         for k in range(4):
             act(A("r16", 16 + 512 * k, 528 + 512 * k), A(R, 512 * k, 512 * k + 512), AF.Copy)
         gathO("r16", 16, 2048, setof("P"), sub(B1, 0, 128))
         cp(PO, sub(B1, 0, 128))
         gather_xs()
+        if last:
+            return
         for k in range(4):
-            c = (B0, B3)[k % 2]
+            c = (B0, B2_)[k % 2]
             mms(c, [(CDP, A("r16", 16 + 512 * k, 528 + 512 * k)), (CDN, A("r16", 15 + 512 * k, 527 + 512 * k))])
             ts(A("m0", 512 * k, 512 * k + 512), c, 0.0, O.is_equal)
         gathO("r16", 16, 2048, setof("cid"), sub(B2_, 0, 128))
@@ -425,7 +427,6 @@ def rank_program(g, core, T, topo):
         for k in range(4):
             act(A("gt", 512 * k, 512 * k + 512), X(A("ks", 2080, 4128), chunks(POS, k, 4)), AF.Copy)
             act(A("g16", 512 * k, 512 * k + 512), A("gt", 512 * k, 512 * k + 512), AF.Copy)
-        gathO("g16", 0, 2048, s0s, sub(B2_, 0, 128))
 
     def s_keys():
         for k in range(4):
@@ -558,13 +559,13 @@ def rank_program(g, core, T, topo):
     for k in range(4):
         act(A("r16", 16 + 512 * k, 528 + 512 * k), A("ra", 512 * k, 512 * k + 512), AF.Copy)
     gathO("r16", 16, 2048, setof("P"), sub(B1, 0, 128))
+    empties()
     cp(PO, sub(B1, 0, 128))
     gather_xs()
     cp(X(A("at"), PO), A("rb"))
     for k in range(4):
         act(A("gt", 512 * k, 512 * k + 512), X(A("bt", 0, 1024), chunks(CQ, k, 4)), AF.Copy)
     act(A("g16"), A("at"), AF.Copy)
-    empties()
     gathO("g16", 0, 2048, s0s, sub(B2_, 256, 384))
     R = ["ra", "rb"]
     gens = []
@@ -585,9 +586,9 @@ def rank_program(g, core, T, topo):
         cp(nc, sub(B1, 16, 32))
         s_keys()
         u_scan()
+        vstep()
         cp(A("uc"), X(A("us"), EU))
         k_scan()
-        vstep()
         for w in range(16):
             mm(sub(B1, 32, 48), bws(w), A("uc", w, 256, 16), w == 0, w == 15)
         lanes_of(A("ks", 0, 2048), ED2)
@@ -636,15 +637,6 @@ def rank_program(g, core, T, topo):
         ts(A("ahl"), A("ai"), F("k128", 1), O.add, 1.0 / 2048, O.mult)
         scan(A("gt", 0, 2048), A("m0"), A("psA"), O.mult, O.max)
         lanes_of(A("gt", 0, 2048), ED2)
-        sel(F("kb0"), 0)
-        sel(F("kb1"), 1)
-        cp(ki, F("kb0"))
-        ts(ki, ki, 127, O.bitwise_and)
-        cp(k2, F("kb1"))
-        ts(k2, k2, 15, O.bitwise_and)
-        bf = F("bf")
-        ts(bf, ki, 16.0, O.mult)
-        tt(bf, bf, k2, O.add)
         vstep()
         if t:
             s_keys()
@@ -659,6 +651,15 @@ def rank_program(g, core, T, topo):
                 mm(A("psB", 64 * k, 64 * k + 64), bws(i), A("df", z0 + i, z0 + 1024, 16), i == 0, i == 15)
         if t:
             new_pos()
+        sel(F("kb0"), 0)
+        sel(F("kb1"), 1)
+        cp(ki, F("kb0"))
+        ts(ki, ki, 127, O.bitwise_and)
+        cp(k2, F("kb1"))
+        ts(k2, k2, 15, O.bitwise_and)
+        bf = F("bf")
+        ts(bf, ki, 16.0, O.mult)
+        tt(bf, bf, k2, O.add)
         for h in (0, 1):
             tt(A("tg", 256 * h, 256 * h + 256), sub(B0, 0, 256), A("ahl", 256 * h, 256 * h + 256), O.add)
         vtr(A("tt"), A("tg"))
@@ -719,8 +720,6 @@ def rank_program(g, core, T, topo):
         cp(ki, F("y"))
         ts(k2, ki, 4, O.arith_shift_right)
         cp(F("sigd"), k2)
-        if t:
-            cp(POS, sub(B2_, 0, 128))
         mer, tmp = F("mer"), F("tmp")
         tt(tmp, F("sigd"), sig, O.min)
         tt(tmp, sub(B1, 112, 128), tmp, O.subtract)
@@ -747,6 +746,11 @@ def rank_program(g, core, T, topo):
         cp(S("su", "bU"), bf)
         cp(A("xbb"), X(A("xa", 0, 2048), S("su", "bU")))
         cp(A("xb", *lanes), A("xbb"))
+        idle, visit, vk = F("idle"), F("visit"), F("vk")
+        tt(tmp, mer, spl, O.add)
+        tt(idle, live, tmp, O.subtract)
+        cp(S("sb", "ib"), idle)
+        prefix(S("sb", "ib"), 16, vk, "pv", sub(B1, 208, 240))
         x1, x2 = S("sh", "x1", 48), S("sh", "x2")
         tt(tmp, mer, dn, O.mult)
         tt(sub(x1, 0, 16), nc, tmp, O.add)
@@ -761,7 +765,9 @@ def rank_program(g, core, T, topo):
         p0, p1, p2 = sub(B0, 0, 256), sub(B0, 256, 512), sub(B3, 0, 256)
         mms(p0, [(M237, xr_), (I16, ckl)])
         gathO("eg16", 0, 256, setof("r8"), sub(B1, 176, 192))
-        gathO("rk", 0, 2048, s0s, sub(B1, 384, 512))
+        if t:
+            gathO("g16", 0, 2048, s0s, sub(B2_, 0, 128))
+        gathO("rk", 0, 2048, s0s, sub(B2_, 384, 512))
         for k in range(4):
             c = (512 * k, 512 * k + 512)
             tt(A("df", *c), X(A("xb"), chunks(CQ, k, 4)), A("xs", *c), O.subtract)
@@ -777,6 +783,21 @@ def rank_program(g, core, T, topo):
         cp(A("bl16"), A("bt", cl, 1024, 4))
         choose(tmp, spl, sub(B1, 176, 192), tl)
         cp(S("su", "eL"), tmp)
+        ts(visit, vk, 95.5, O.is_lt)
+        tt(visit, visit, idle, O.mult)
+        ts(tl, lane, 96.0, O.add)
+        choose(tmp, visit, vk, tl)
+        cp(S("su", "vL"), tmp)
+        cp(X(A("vs"), S("su", "vL")), A("xsb"))
+        q = T.cores[(rank + 1 + t % 7) % 8]
+        h = T.cores[(rank - 1 - t % 7) % 8]
+        send(q, "in%d" % t, A("vs", 0, 96), "ra%d" % t, "la%d" % t)
+        ts(tl, lane, 2048.0, O.add)
+        choose(tmp, visit, sf, tl)
+        cp(S("su", "vA"), tmp)
+        cp(A("res", 96, 352), A("xsb"))
+        if t:
+            cp(POS, sub(B2_, 0, 128))
         for k in range(4):
             c = (512 * k, 512 * k + 512)
             ts(A("g16", *c), A("psA", *c), 0.0, O.is_lt)
@@ -789,7 +810,7 @@ def rank_program(g, core, T, topo):
         tt(nl, nl, spl, O.mult)
         cv, lv, cql, rp = F("cv", 128), F("lv", 128), F("cql", 128), F("rp", 128)
         rkO, rlO = F("rkO", 128), F("rlO", 128)
-        cp(rkO, sub(B1, 384, 512))
+        cp(rkO, sub(B2_, 384, 512))
         cp(x2, nl)
         for w in range(16):
             mm(sub(p2, w, 256, 16), ors(w), x2)
@@ -803,6 +824,7 @@ def rank_program(g, core, T, topo):
         tt(cv, cv, lv, O.mult)
         tt(cql, cv, CQF, O.add)
         cp(S("su", "cqL", 128), cql)
+        gathO("bl16", 0, 256, setof("np"), sub(B2_, 192, 208))
         cp(A("bt", cl, 1024, 4), p0)
         cp(A("bt", 1024, 1280), p2)
         cp(A("lft"), p2)
@@ -816,10 +838,12 @@ def rank_program(g, core, T, topo):
         for k in range(4):
             act(A("gt", 512 * k, 512 * k + 512), X(A("bt", 0, 1280), chunks(S("su", "cqL", 128), k, 4)), AF.Copy)
         cp(A("g16"), X(A("bt", 0, 1280), S("su", "cqL", 128)))
-        gathO("g16", 0, 2048, setof("np"), sub(B3, 256, 384))
         mms(p0, [(M237, xr_), (M237N, xl_), (I16, ckl)])
         mms(p1, [(M237, xl_), (I16, A("eg16"))])
-        gathO("bl16", 0, 256, setof("np"), sub(B2_, 192, 208))
+        gathO("g16", 0, 2048, setof("np"), sub(B3, 256, 384))
+        cp(A("sz", cl, 1024, 4), p0)
+        cp(A("sze"), p1)
+        cp(X(A("sz"), S("su", "eL")), A("sze"))
         agents()
         ts(rlO, sub(B1, 256, 384), 0.0625, O.mult)
         tt(rp, rkO, rlO, O.subtract)
@@ -829,28 +853,10 @@ def rank_program(g, core, T, topo):
         tt(rp, rp, rlO, O.add)
         stc = F("stc")
         cp(stc, sub(B2_, 192, 208))
-        idle, visit, vk = F("idle"), F("visit"), F("vk")
-        tt(tmp, mer, spl, O.add)
-        tt(idle, live, tmp, O.subtract)
-        cp(S("sb", "ib"), idle)
-        prefix(S("sb", "ib"), 16, vk, "pv", sub(B1, 208, 240))
-        ts(visit, vk, 95.5, O.is_lt)
-        tt(visit, visit, idle, O.mult)
-        ts(tl, lane, 96.0, O.add)
-        choose(tmp, visit, vk, tl)
-        cp(S("su", "vL"), tmp)
-        cp(X(A("vs"), S("su", "vL")), A("xsb"))
-        ts(tl, lane, 2048.0, O.add)
-        choose(tmp, visit, sf, tl)
-        cp(S("su", "vA"), tmp)
         tt(stc, stc, rnk, O.add)
+        ts(tl, lane, 2048.0, O.add)
         choose(tmp, visit, stc, tl)
         cp(S("su", "vP"), tmp)
-        q = T.cores[(rank + 1 + t % 7) % 8]
-        h = T.cores[(rank - 1 - t % 7) % 8]
-
-        send(q, "in%d" % t, A("vs", 0, 96), "ra%d" % t, "la%d" % t)
-        cp(A("res", 96, 352), A("xsb"))
         tt(rp, rp, sub(B3, 256, 384), O.add)
         cp(S("su", "npL", 128), rp)
         if t < 3:
@@ -861,14 +867,11 @@ def rank_program(g, core, T, topo):
             act(A("ks", 2080, 4128), A("psA"), AF.Copy)
         tt(X(A(R[1]), S("su", "npL", 128)), A("gt", 0, 2048), A(R[0]), O.add)
         R = R[::-1]
-        cp(A("sz", cl, 1024, 4), p0)
-        cp(A("sze"), p1)
-        cp(X(A("sz"), S("su", "eL")), A("sze"))
-        if t < 3:
-            empties()
-        order_tables(R[0])
         gens[:] = [visits(t, q, h)]
         vstep()
+        if t < 3:
+            empties()
+        order_tables(R[0], t == 3)
         if t < 3:
             mt = S("sb", "mt")
             cp(mt, mer)

from concourse.mybir import AluOpType as O, ActivationFunctionType as AF, AxisListType as AX

F4, B2, H2, I4, U2 = "float32", "bfloat16", "float16", "int32", "uint16"
SCRATCH = {}
for _n, _w, _d in [
        ("xa", 2304, B2), ("xc", 2304, B2), ("xs", 2304, B2), ("ra", 2048, F4), ("rb", 2048, F4), ("r16", 2064, H2),
        ("at", 2048, F4), ("bt", 1536, F4), ("sz", 1536, F4), ("el", 1280, F4), ("ks", 4128, F4),
        ("gt", 2048, F4), ("g16", 2048, H2), ("df", 2048, B2), ("xr", 2048, B2), ("zb", 2048, B2), ("sqs", 2048, B2),
        ("eq", 1024, B2), ("bw", 2048, B2), ("sets", 14336, H2), ("wts", 2048, B2), ("orp", 2048, H2),
        ("mlt", 1024, I4), ("act", 1024, I4), ("d0", 1024, B2), ("ck16", 1024, H2),
        ("mr", 1536, B2), ("ones", 512, B2), ("us", 2048, B2), ("rl", 2048, B2), ("m0", 2048, B2), ("rk", 2048, H2),
        ("bt16", 1024, H2), ("xl", 1024, B2), ("xb", 1024, B2), ("wm", 3968, H2), ("wb", 1664, B2),
        ("xsb", 256, B2), ("xbb", 256, B2), ("uc", 256, B2), ("ud", 256, B2), ("uv", 256, B2), ("acq", 256, U2), ("ai", 512, I4),
        ("ahl", 512, F4), ("mrb", 512, B2), ("tg", 512, F4), ("tt", 512, F4),
        ("ag16", 256, H2), ("eg16", 256, H2), ("drep", 256, H2), ("x16", 1024, H2), ("bl16", 256, H2), ("lt16", 256, H2),
        ("dvt", 256, F4), ("lft", 256, F4), ("sze", 256, F4), ("zd", 256, F4), ("ctr", 256, F4),
        ("vs", 352, B2), ("res", 352, B2), ("vag", 96, H2), ("yv", 96, B2), ("ri", 96, I4), ("nx", 256, B2),
        ("sm", 2800, F4), ("si", 416, I4), ("su", 1120, U2), ("sh", 288, H2), ("sb", 160, B2), ("lim", 2, I4), ("wtc", 1, I4)]:
    SCRATCH[_n] = ("sbuf", [128, _w], _d)
for _t in range(4):
    SCRATCH["in%d" % _t] = ("sbuf", [128, 96], B2)
    SCRATCH["ry%d" % _t] = ("sbuf", [128, 96], B2)
SCRATCH["psA"] = ("psum", [128, 2048], F4)
SCRATCH["psB"] = ("psum", [128, 2048], F4)
SEMAPHORES = ["sv", "ss", "st", "sg"] + ["d%d" % i for i in range(12)]
for _t in range(4):
    SEMAPHORES += ["ra%d" % _t, "rb%d" % _t, "la%d" % _t, "lb%d" % _t]
BIG = 33554432.0


def rank_program(g, core, T, topo):
    rank = T.rank_of(core)
    if rank is None:
        return
    Q = {"v": g.vector, "s": g.scalar, "t": g.tensor, "g": g, "y": g.sync}
    SEM = {"v": "sv", "s": "ss", "t": "st", "g": "sg"}
    cnt = {"v": 0, "s": 0, "t": 0, "g": 0}
    know = {e: {} for e in Q}
    hist = {}
    recs = {}

    def A(n, a=0, b=None, s=1):
        return (n, a, SCRATCH[n][1][1] if b is None else b, s)

    def X(w, o):
        return ("X", w, o, 0)

    def ap(x):
        if not isinstance(x, tuple):
            return x
        if x[0] == "X":
            return ap(x[1]).indirect(ap(x[2]))
        n, a, b, s = x
        return T[n][:, a:b] if s == 1 else T[n][:, a:b:s]

    def sub(x, a, b, s=1):
        return (x[0], x[1] + a, x[1] + b, s)

    def touch(e, outs, ins, seq_e):
        acc = []
        for x, w in [(o, True) for o in outs] + [(i, False) for i in ins]:
            if not isinstance(x, tuple):
                continue
            for y, ww in ([(x[1], w), (x[2], False)] if x[0] == "X" else [(x, w)]):
                n, a, b, s = y
                if n[:2] == "ps":
                    for k in range(a // 512, (b - 1) // 512 + 1):
                        acc.append((n, 512 * k, 512 * k + 512, True, True))
                else:
                    acc.append((n, a, b, ww, False))
        need = {}
        for n, a, b, w, ps in acc:
            for r in recs.get(n, []):
                if r[0] < b and a < r[1] and (w or r[4]) and not (r[2] == seq_e[0] and r[2][0] == "D") and not (ps and r[2] == e and e == "t"):
                    need[r[2]] = max(need.get(r[2], 0), r[3])
        for x in sorted(need):
            if know[e].get(x, 0) < need[x]:
                Q[e].wait_ge(T.sem[SEM[x]], need[x])
                for k, v in hist[(x, need[x])].items():
                    know[e][k] = max(know[e].get(k, 0), v)
                know[e][x] = need[x]
        who, seq = seq_e
        hist[(who, seq)] = dict(know[e])
        for n, a, b, w, ps in acc:
            L = recs.setdefault(n, [])
            if w:
                L[:] = [r for r in L if not (a <= r[0] and r[1] <= b)]
                L.append([a, b, who, seq, True])
            else:
                for r in L:
                    if r[0] == a and r[1] == b and r[2] == who and not r[4]:
                        r[3] = seq
                        break
                else:
                    L.append([a, b, who, seq, False])

    def emit(e, fn, outs, ins):
        cnt[e] += 1
        touch(e, outs, ins, (e, cnt[e]))
        fn().then_inc(T.sem[SEM[e]], 1)

    def cp(out, i, e="v"):
        if e == "s":
            act(out, i, AF.Copy)
        else:
            emit("v", lambda: g.vector.tensor_copy(ap(out), ap(i)), [out], [i])

    def tt(out, a, b, op):
        emit("v", lambda: g.vector.tensor_tensor(ap(out), ap(a), ap(b), op), [out], [a, b])

    def ts(out, a, s1, op0, s2=None, op1=None):
        if op1 is None:
            emit("v", lambda: g.vector.tensor_scalar(ap(out), ap(a), ap(s1), None, op0), [out], [a, s1])
        else:
            emit("v", lambda: g.vector.tensor_scalar(ap(out), ap(a), ap(s1), ap(s2), op0, op1), [out], [a, s1, s2])

    def scan(out, d0, d1, op0, op1):
        emit("v", lambda: g.vector.tensor_tensor_scan(ap(out), ap(d0), ap(d1), 0.0, op0, op1), [out], [d0, d1])

    def vtr(out, i):
        emit("v", lambda: g.vector.transpose(ap(out), ap(i)), [out], [i])

    def ms(out, c):
        emit("v", lambda: g.vector.memset(ap(out), c), [out], [])

    def act(out, i, f, scale=1.0):
        emit("s", lambda: g.scalar.activation(ap(out), ap(i), f, scale=ap(scale)), [out], [i, scale])

    def mm(out, l, r, start=True, stop=True):
        emit("t", lambda: g.tensor.matmul(ap(out), ap(l), ap(r), start, stop), [out], [l, r])

    def mms(out, pairs):
        for k, (l, r) in enumerate(pairs):
            mm(out, l, r, k == 0, k == len(pairs) - 1)

    def asel(out, i, pat, op, base, cm):
        emit("g", lambda: g.affine_select(ap(out), ap(i), pat, op, 0.0, base, cm), [out], [i])

    def iota(out, pat, base, cm):
        emit("g", lambda: g.iota(ap(out), pat, base, cm, allow_small_or_imprecise_dtypes=True), [out], [])

    nd = [0]

    def dmas(e, pairs):
        who = "D%d" % nd[0]
        SEM[who] = "d%d" % nd[0]
        nd[0] += 1
        for k, (o, i, oa, ia) in enumerate(pairs):
            touch(e, [o] if o else [], [i] if i else [], (who, 16 * len(pairs)))
            Q[e].dma_start(oa, ia).then_inc(T.sem[SEM[who]], 16)
        return who, 16 * len(pairs)

    fin = []
    slots = {}
    used = {"sm": 0, "si": 0, "su": 0, "sh": 0, "sb": 0}

    def S(buf, name, w=16):
        if (buf, name) not in slots:
            slots[(buf, name)] = A(buf, used[buf], used[buf] + w)
            used[buf] += (w + 15) // 16 * 16
        return slots[(buf, name)]

    def F(name, w=16):
        return S("sm", name, w)

    for n, src in (("mlt", T.ml), ("xa", T.x0), ("act", T.ac), ("lim", T.lims), ("wtc", T.wt)):
        w = src.shape[1]
        fin.append(dmas("y" if n != "act" else "s", [(A(n, 0, w), None, T[n][:, 0:w], src[:, 0:w])]))

    ms(A("ones"), 1.0)
    ms(A("rl"), 1.0)
    iota(F("i16"), [[1, 16]], 0, 0)
    iota(F("pi", 1), [[0, 1]], 0, 1)
    cp1 = A("el", 0, 1024)
    iota(cp1, [[1, 1024]], 1, 0)
    iota(F("l16"), [[16, 16]], 0, 0)
    iota(F("c64", 64), [[16, 64]], 0, 0)
    m8 = A("tg", 384, 512)
    iota(m8, [[1, 128]], 0, 0)
    wb = {}

    def W1(name, buf="wb"):
        k = (buf, name)
        if k not in wb:
            i = len([1 for z in wb if z[0] == buf])
            wb[k] = A(buf, 128 * i, 128 * i + 128)
        return wb[k]

    o128 = A("ones", 0, 128)
    BB, ID, SP, SN, TW = W1("BB"), W1("ID"), W1("SP"), W1("SN"), W1("TW")
    asel(BB, o128, [[-16, 8], [0, 16]], O.is_ge, 0, 1)
    asel(BB, BB, [[16, 8], [0, 16]], O.is_ge, 15, -1)
    asel(ID, o128, [[-1, 128]], O.is_equal, 0, 1)
    asel(A("bw"), A("rl"), [[1, 16], [0, 8], [-1, 16]], O.is_equal, 0, 0)
    asel(A("bw"), A("bw"), [[0, 16], [-16, 8], [0, 16]], O.is_ge, 0, 1)
    asel(A("bw"), A("bw"), [[0, 16], [16, 8], [0, 16]], O.is_ge, 15, -1)
    asel(SP, o128, [[-1, 128]], O.is_equal, 16, 1)
    asel(SN, o128, [[-1, 128]], O.is_equal, -16, 1)
    asel(TW, BB, [[1, 128]], O.is_gt, 0, -1)
    iota(A("rb"), [[1, 2048]], 0, 0)
    pi = S("si", "pi", 1)
    kcol, mO, mE = F("kcol", 1), F("mO", 1), F("mE", 1)
    cp(pi, F("pi", 1))
    ts(S("si", "p2", 1), pi, 15, O.bitwise_and)
    cp(kcol, S("si", "p2", 1))
    ts(S("si", "p2", 1), pi, 4, O.arith_shift_right, 1, O.bitwise_and)
    cp(mO, S("si", "p2", 1))
    ts(mE, mO, -1.0, O.mult, 1.0, O.add)
    ts(F("mE4", 1), mE, 4096.0, O.mult)
    ts(F("mO4", 1), mO, 4096.0, O.mult)
    ts(F("k128", 1), kcol, 128.0, O.mult)
    ts(F("k11", 1), kcol, -11.0, O.add)
    rm = F("rm")
    ts(rm, F("i16"), kcol, O.is_equal)

    def RM(r):
        return sub(rm, r, r + 1)

    def coef(name, terms):
        c = F("c_" + name, 1)
        r0, w0 = terms[0]
        ts(c, RM(r0), float(w0), O.mult)
        for r, w in terms[1:]:
            ts(F("c_t", 1), RM(r), float(w), O.mult)
            tt(c, c, F("c_t", 1), O.add)
        return c

    lane, c4 = F("lane"), F("c4", 64)
    ts(lane, F("l16"), kcol, O.add)
    ts(c4, F("c64", 64), kcol, O.add)
    ts(S("sb", "tri"), F("i16"), kcol, O.is_gt)
    ci, ck0, ck1 = A("ai"), A("ks", 0, 512), A("ks", 512, 1024)
    for h in (0, 1):
        cpart = A("el", 512 * h, 512 * h + 512)
        ts(ck0, cpart, -1.0, O.add)
        cp(ci, ck0)
        ts(ci, ci, 3, O.bitwise_and)
        ts(ck1, ci, F("k11", 1), O.is_equal)
        ts(ck0, ck0, RM(8), O.mult)
        tt(A("ck16", 512 * h, 512 * h + 512), ck0, ck1, O.add)
    ts(A("d0"), A("rl", 0, 1024), RM(2), O.mult)

    def mk(name, src, col, w=1.0, buf="wm"):
        m = W1(name, buf)
        ts(m, src, col, O.mult, float(w), O.mult)
        return m

    one = F("one1", 1)
    ms(one, 1.0)
    I16 = mk("I16", ID, one)
    mi = S("si", "mi", 128)
    par, ta, tb = A("tg", 256, 384), A("tg", 0, 128), A("tg", 128, 256)
    cp(mi, m8)
    ts(mi, mi, 15, O.bitwise_and)
    ts(ta, mi, 2.0, O.is_equal)
    for r in (3.0, 7.0):
        ts(tb, mi, r, O.is_equal)
        tt(ta, ta, tb, O.add)
    BB237 = W1("BB237", "wb")
    tt(BB237, BB, ta, O.mult)
    ts(A("us", 0, 1024), A("mlt"), 2048.0, O.is_lt)
    for k in range(2):
        mms(A("psB", 512 * k, 512 * k + 512), [(BB237, A("us", 512 * k, 512 * k + 512)), (I16, A("ck16", 512 * k, 512 * k + 512))])
    cp(A("sz", 0, 1024), A("psB", 0, 1024))
    scan(A("bt", 0, 1024), A("d0"), A("sz", 0, 1024), O.mult, O.add)
    cp(A("bt16"), A("bt", 0, 1024))
    cp(A("lt16"), A("bt", 0, 1024, 4))
    ms(A("ks", 0, 2048), 0.0)
    names = ["E", "n", "r8", "cid", "P", "np", "st"]
    terms = [[(2, 1), (3, -1), (6, 1), (7, 1)], [(7, 1)], [(8, 1)], [(1, 1)], [(0, 16), (10, 1)], [(2, 1), (3, -1), (5, 1)], [(2, 1), (3, -1), (6, 1)]]
    ccol = {}

    def setof(name):
        i = names.index(name)
        return lambda w: A("sets", 2048 * i + 128 * w, 2048 * i + 128 * w + 128)
    for i, nm in enumerate(names):
        ccol[nm] = coef(nm, terms[i])
    for nm in ("np", "n", "cid", "P", "E", "r8", "st"):
        i = names.index(nm)
        act(A("sets", 2048 * i, 2048 * i + 2048), A("bw"), AF.Copy, ccol[nm])
    wf = F("wf", 1)
    cp(wf, A("wtc"))
    act(A("wts"), A("bw"), AF.Copy, wf)

    def bws(w):
        return A("bw", 128 * w, 128 * w + 128)

    s0s = setof("cid")

    def wtw(w):
        return A("wts", 128 * w, 128 * w + 128)

    def ors(w):
        return A("orp", 128 * w, 128 * w + 128)
    for w in range(16):
        ts(ors(w), BB, RM(w), O.mult)

    PE_, PO_, P01, P10 = mk("PE", ID, mE), mk("PO", ID, mO), mk("P01", SP, mE), mk("P10", SN, mO)
    BBK, BBS, BBN = mk("BBK", BB, one, 2048.0, "wb"), mk("BBS", BB, one, -8.0, "wb"), mk("BBN", BB, one, -1.0, "wb")
    RKS, RKB = mk("RKS", BB, RM(0), -0.5), mk("RKB", BB, RM(0), -128.0)
    BB16 = mk("BB16", BB, one)
    RPS = mk("RPS", BB, coef("ks", [(0, 2.0 ** -8), (10, 2.0 ** -12), (9, 2048)]))
    CDP, CDN = mk("CDP", BB, RM(1)), mk("CDN", BB, RM(1), -1.0)
    STR, NRP = mk("STR", BB, ccol["st"]), mk("NRP", BB, ccol["n"])
    CLS = [mk("CLS%d" % m, BB, RM(11 + m), 64.0, "wb") for m in range(4)]
    ts(mi, mi, 1, O.bitwise_and)
    cp(par, mi)
    RPB = W1("RPB", "wm")
    ts(ta, BB, coef("kb1", [(10, 1.0), (0, -1.0)]), O.mult)
    tt(ta, ta, par, O.mult)
    ts(tb, BB, coef("kb2", [(0, 1.0), (9, 2048.0)]), O.mult)
    tt(RPB, ta, tb, O.add)

    def rowmap(name, src, rows, w=1.0):
        m = W1(name, "wm")
        ts(ta, bws(rows[0]), RM(src), O.mult, float(w), O.mult)
        for r in rows[1:]:
            ts(tb, bws(r), RM(src), O.mult, float(w), O.mult)
            tt(ta, ta, tb, O.add)
        cp(m, ta)
        return m
    M237, M237N, M7N = rowmap("M237", 0, [2, 3, 7]), rowmap("M237N", 0, [2, 3, 7], -1), rowmap("M7N", 0, [7], -1)
    M5, M1N, M81, M81N, M56 = rowmap("M5", 0, [5]), rowmap("M1N", 0, [1], -1), rowmap("M81", 8, [1]), rowmap("M81N", 8, [1], -1), rowmap("M56", 0, [5, 6])
    M567 = W1("M567", "wm")
    tt(M567, M7N, M56, O.add)
    ts(M567, M567, -1.0, O.mult)
    I23 = mk("I23", ID, coef("i23", [(2, 1), (3, 1)]))
    IX = W1("IX", "wm")
    tt(IX, I16, M81, O.add)
    RPP = mk("RPP", BB, ccol["P"])
    H0, PX10, H10, C1 = rowmap("H0", 0, [0]), W1("PX10", "wm"), rowmap("H10", 0, [10], -16), rowmap("C1", 0, [1])
    cp(PX10, bws(10))
    ms(A("mr"), 1.0)
    ms(A("mr", 0, 1536, 16), 0.0)
    ms(A("mrb"), 0.0)
    ms(A("mrb", 0, 512, 16), BIG)
    for n in ("zb", "eq", "xl", "xb"):
        ms(A(n), 0.0)
    ms(A("vs"), 0.0)
    ms(A("zd"), 0.0)
    ms(F("neg"), -1.0)
    cp(A("r16", 0, 16), F("neg"))
    lims = F("lims", 2)
    cp(lims, A("lim"))
    limz = F("limz", 1)
    cp(limz, sub(lims, 0, 1))

    def gathO(src, a, n, st, out):
        for w in range(16):
            mm(out, st(w), A(src, a + w, a + n, 16), w == 0, w == 15)

    def s2o(r1, out, n):
        mms(sub(out, 0, n, 2), [(PE_, sub(r1, 0, n, 2)), (P01, sub(r1, 1, n, 2))])
        mms(sub(out, 1, n, 2), [(P10, sub(r1, 0, n, 2)), (PO_, sub(r1, 1, n, 2))])

    def lanes_of(win, dup):
        cp(A("tg"), X(win, dup))
        vtr(A("tt"), A("tg"))

    def sel(out, r, me=mE, mo=mO):
        ts(F("selA"), A("tt", r, 512, 32), me, O.mult)
        ts(F("selB"), A("tt", 16 + r, 512, 32), mo, O.mult)
        tt(out, F("selA"), F("selB"), O.add)

    def prefix(ind, n, out, tag, ps):
        mm(sub(ps, 0, n), TW, ind)
        mm(sub(ps, n, 2 * n), BB, ind)
        cp(F(tag + "tot", n), sub(ps, n, 2 * n))
        inc = F(tag + "inc", n)
        scan(inc, A("ones", 0, n), F(tag + "tot", n), O.mult, O.add)
        tt(out, inc, F(tag + "tot", n), O.subtract)
        tt(out, out, sub(ps, 0, n), O.add)
        return sub(inc, n - 1, n)

    def lt(name):
        return F(name)

    def choose(out, cond, a, b, tmp="chT", w=16):
        d = F(tmp + str(w), w)
        tt(d, a, b, O.subtract)
        tt(d, d, cond, O.mult)
        tt(out, d, b, O.add)

    B0, B1, B2_, B3 = [A("psB", 512 * k, 512 * k + 512) for k in range(4)]
    PO, CQ, CQF = S("su", "po", 128), S("su", "cq", 128), F("cqf", 128)

    def chunks(off, k, n):
        w = (off[2] - off[1]) // n
        return sub(off, k * w, k * w + w)

    def order_tables(R, last):
        for k in range(4):
            act(A("r16", 16 + 512 * k, 528 + 512 * k), A(R, 512 * k, 512 * k + 512), AF.Copy)
        gathO("r16", 16, 2048, setof("P"), sub(B1, 0, 128))
        cp(PO, sub(B1, 0, 128))
        gather_xs()
        if last:
            return
        for k in range(4):
            c = (B0, B2_)[k % 2]
            mms(c, [(CDP, A("r16", 16 + 512 * k, 528 + 512 * k)), (CDN, A("r16", 15 + 512 * k, 527 + 512 * k))])
            ts(A("m0", 512 * k, 512 * k + 512), c, 0.0, O.is_equal)
        gathO("r16", 16, 2048, setof("cid"), sub(B2_, 0, 128))
        cp(CQF, sub(B2_, 0, 128))
        cp(CQ, CQF)
        scan(A("rk"), A("m0"), A("m0"), O.mult, O.add)

    def gather_xs():
        cp(A("xs", 1024, 2048), X(A("xa", 0, 2048), chunks(PO, 1, 2)))
        for k in range(2):
            act(A("xs", 512 * k, 512 * k + 512), X(A("xa", 0, 2048), chunks(PO, k, 4)), AF.Copy)

    POS = S("su", "pos", 128)

    def agents():
        for k in range(4):
            act(A("at", 512 * k, 512 * k + 512), X(A("gt", 0, 2048), chunks(POS, k, 4)), AF.Copy)

    def build_xc(m):
        act(A("rl"), A("at"), AF.Copy)
        for k in range(4):
            c = (B0, B3)[k % 2]
            mms(c, [(ID, A("xa", 512 * k, 512 * k + 512)), (CLS[m], A("rl", 512 * k, 512 * k + 512))])
            act(A("xc", 512 * k, 512 * k + 512), c, AF.Copy)

    def new_pos():
        for k in range(4):
            act(A("gt", 512 * k, 512 * k + 512), X(A("ks", 2080, 4128), chunks(POS, k, 4)), AF.Copy)
            act(A("g16", 512 * k, 512 * k + 512), A("gt", 512 * k, 512 * k + 512), AF.Copy)

    def s_keys():
        for k in range(4):
            mm(A("psA", 512 * k, 512 * k + 512), RKS, A("rk", 512 * k, 512 * k + 512), True, False)
            mm(A("psA", 512 * k, 512 * k + 512), RPS, A("r16", 16 + 512 * k, 528 + 512 * k), False, False)
        for k in range(4):
            mm(A("psA", 512 * k, 512 * k + 512), BBS, A("xs", 512 * k, 512 * k + 512), False, True)

    def u_scan():
        scan(A("us"), A("m0"), A("xs", 0, 2048), O.mult, O.max)

    def k_scan():
        scan(A("ks", 0, 2048), A("m0"), A("psA"), O.mult, O.max)

    def empties():
        act(A("bt16"), A("sz", 0, 1024), AF.Copy)
        gathO("bt16", 0, 1024, setof("n"), sub(B2_, 0, 64))
        e64, r64 = F("e64", 64), F("r64", 64)
        ts(e64, sub(B2_, 0, 64), 0.5, O.is_lt)
        cp(S("sb", "e64", 64), e64)
        e = prefix(S("sb", "e64", 64), 64, r64, "pe", sub(B2_, 64, 192))
        cp(F("ecnt", 1), e)
        ts(F("t64", 64), c4, 256.0, O.add)
        ts(F("u64", 64), r64, 255.5, O.is_lt)
        tt(e64, e64, F("u64", 64), O.mult)
        choose(r64, e64, r64, F("t64", 64), "ch64", 64)
        cp(S("su", "l64", 64), r64)
        cp(X(A("el"), S("su", "l64", 64)), A("ck16"))

    def send(dst, out, src, rs, ls):
        rid, pid, _ = topo.addr(dst)
        es = topo.engines(core, dst)[:4]
        m = 0
        for e in es:
            m |= 1 << e
        SEM[ls] = ls
        touch("g", [], [src], (ls, len(es)))
        g.remote_dma(out_ap=T[out][:], in_ap=ap(src), remote_sem=T.sem[rs], local_sem=T.sem[ls], pid=pid, routing_id=rid, dma_engine_mask=m)
        fin.append((ls, len(es)))

    def arrived(buf, rs, src):
        n = len(topo.engines(src, core)[:4])
        SEM[rs] = rs
        hist[(rs, n)] = {}
        recs.setdefault(buf, []).append([0, 96, rs, n, True])
        fin.append((rs, n))

    def visits(t, q, h):
        IN = "in%d" % t
        arrived(IN, "ra%d" % t, h)
        for w in range(16):
            mm(sub(B3, 0, 6), wtw(w), A(IN, w, 96, 16), w == 0, w == 15)
        vi = S("si", "vi", 6)
        cp(vi, sub(B3, 0, 6))
        ts(vi, vi, 2047, O.bitwise_and)
        cp(S("su", "vi", 6), vi)
        cp(A("vag"), X(A("at"), S("su", "vi", 6)))
        mm(sub(B3, 16, 112), STR, A("vag"))
        mm(sub(B3, 112, 208), NRP, A("vag"))
        cp(A("zb", 0, 1536, 16), A(IN))
        scan(A("xr", 0, 1536), A("mr", 0, 1536), A("zb", 0, 1536), O.mult, O.add)
        yield
        hl = F("hl", 96)
        ts(hl, sub(B3, 112, 208), -1.0, O.add, kcol, O.min)
        tt(hl, hl, sub(B3, 16, 112), O.add)
        cp(S("su", "hl", 96), hl)
        hx = A("sqs", 0, 1536)
        tt(hx, X(A("xs", 0, 2048), S("su", "hl", 96)), A("xr", 0, 1536), O.subtract)
        act(hx, hx, AF.Square)
        for w in range(16):
            mm(sub(B3, 208, 214), setof("st")(w), A("vag", w, 96, 16), w == 0, w == 15)
        for i in range(16):
            mm(sub(B0, 256, 352), bws(i), A("sqs", i, 1536, 16), i == 0, i == 15)
        yield
        ts(A("tg", 0, 96), sub(B0, 256, 352), 16.0, O.mult, kcol, O.add)
        vtr(A("tt", 0, 96), A("tg", 0, 96))
        scan(A("tg", 0, 96), A("mrb", 0, 96), A("tt", 0, 96), O.max, O.min)
        k6 = S("si", "k6", 6)
        cp(k6, A("tg", 15, 96, 16))
        ts(k6, k6, 15, O.bitwise_and)
        cp(S("sh", "k6", 6), k6)
        s2o(S("sh", "k6", 6), sub(B3, 224, 230), 6)
        yield
        y6 = F("y6", 6)
        cp(y6, sub(B3, 224, 230))
        tt(y6, y6, sub(B3, 208, 214), O.add)
        cp(S("su", "y6", 6), y6)
        cp(A("yv"), X(A("xs", 0, 2048), S("su", "y6", 6)))
        send(h, "ry%d" % t, A("yv"), "rb%d" % t, "lb%d" % t)
        yield
        arrived("ry%d" % t, "rb%d" % t, q)
        tt(A("ri"), A("ry%d" % t), A("vs", 0, 96), O.add)
        ts(A("ri"), A("ri"), 1, O.arith_shift_right)
        cp(A("res", 0, 96), A("ri"))
        cp(A("nx"), X(A("res"), S("su", "vL")))
        cp(X(A("xa"), S("su", "vA")), A("nx"))
        if t < 3:
            cp(X(A("xs"), S("su", "vP")), A("nx"))
            cp(X(A("xc"), S("su", "vA")), A("nx"))
        yield

    gathO("bt16", 0, 1024, setof("np"), sub(B2_, 0, 64))
    gathO("bt16", 0, 1024, setof("n"), sub(B2_, 64, 128))
    t64, u64 = F("t64", 64), F("u64", 64)
    ts(t64, c4, 2048.0, O.add)
    ts(u64, sub(B2_, 64, 128), 0.5, O.is_gt)
    s64 = F("s64", 64)
    cp(s64, sub(B2_, 0, 64))
    choose(s64, u64, s64, t64, "ch64", 64)
    cp(S("su", "l64", 64), s64)
    cp(X(A("ks", 0, 3072), S("su", "l64", 64)), cp1)
    ts(A("m0"), A("ks", 0, 2048), 0.0, O.is_equal)
    scan(A("g16"), A("m0"), A("ks", 0, 2048), O.mult, O.add)
    ms(A("el"), 0.0)
    r91 = coef("r91", [(9, 1), (1, -1)])
    gathO("g16", 0, 2048, s0s, sub(B2_, 0, 128))
    ts(CQF, sub(B2_, 0, 128), -1.0, O.add)
    cp(CQ, CQF)
    scan(A("rk"), A("m0"), A("m0"), O.mult, O.add)
    ts(A("rl"), A("rk"), kcol, O.is_equal)
    for k in range(4):
        c = (512 * k, 512 * k + 512)
        px = A("r16", 16 + 512 * k, 528 + 512 * k)
        tt(px, X(A("mlt"), chunks(CQ, k, 4)), A("rl", *c), O.mult)
        mm(A("psA", *c), BB16, px)
        ts(A("ai"), A("psA", *c), 0.0625, O.mult, -0.46875, O.add)
        cp(A("bt16", 0, 512), A("ai"))
        mms(A("psB", *c), [(H0, A("bt16", 0, 512)), (PX10, px), (H10, A("bt16", 0, 512)), (C1, A("g16", *c))])
        ts(A("ra", *c), A("psB", *c), r91, O.add)
    for k in range(4):
        act(A("r16", 16 + 512 * k, 528 + 512 * k), A("ra", 512 * k, 512 * k + 512), AF.Copy)
    gathO("r16", 16, 2048, setof("P"), sub(B1, 0, 128))
    empties()
    cp(PO, sub(B1, 0, 128))
    gather_xs()
    cp(X(A("at"), PO), A("rb"))
    for k in range(4):
        act(A("gt", 512 * k, 512 * k + 512), X(A("bt", 0, 1024), chunks(CQ, k, 4)), AF.Copy)
    act(A("g16"), A("at"), AF.Copy)
    gathO("g16", 0, 2048, s0s, sub(B2_, 256, 384))
    R = ["ra", "rb"]
    gens = []

    def vstep():
        if gens:
            next(gens[0])

    for t in range(4):
        cl = t
        lanes = (cl, 1024, 4)
        gathO("lt16", 0, 256, setof("E"), sub(B1, 0, 16))
        gathO("lt16", 0, 256, setof("n"), sub(B1, 16, 32))
        EU, ED2 = S("su", "eu"), S("su", "ed2", 32)
        nc = F("nc")
        for o in (EU, sub(ED2, 0, 32, 2), sub(ED2, 1, 32, 2)):
            ts(o, sub(B1, 0, 16), -1.0, O.add)
        cp(nc, sub(B1, 16, 32))
        s_keys()
        u_scan()
        vstep()
        cp(A("uc"), X(A("us"), EU))
        k_scan()
        for w in range(16):
            mm(sub(B1, 32, 48), bws(w), A("uc", w, 256, 16), w == 0, w == 15)
        lanes_of(A("ks", 0, 2048), ED2)
        sel(F("key"), 0, F("mE4", 1), F("mO4", 1))
        ki, k2 = S("si", "ki"), S("si", "k2")
        sf, hf, sig, rnk = F("sf"), F("hf"), F("sig"), F("rnk")
        cp(ki, F("key"))
        ts(k2, ki, 2047, O.bitwise_and)
        cp(sf, k2)
        cp(S("su", "sU"), k2)
        ts(k2, ki, 1023, O.bitwise_and)
        cp(S("su", "hU"), k2)
        cp(A("acq"), X(A("act"), S("su", "hU")))
        cp(A("xsb"), X(A("xa", 0, 2048), S("su", "sU")))
        cp(A("xl", *lanes), A("xsb"))
        for k in range(4):
            c = (512 * k, 512 * k + 512)
            mm(A("psA", *c), RKB, A("rk", *c), True, False)
            mm(A("psA", *c), RPB, A("r16", 16 + 512 * k, 528 + 512 * k), False, False)
            tt(A("df", *c), X(A("xl"), chunks(CQ, k, 4)), A("xs", *c), O.subtract)
            act(A("sqs", *c), A("df", *c), AF.Square)
        vstep()
        for k in range(4):
            mm(A("psA", 512 * k, 512 * k + 512), BBK, A("sqs", 512 * k, 512 * k + 512), False, True)
        ts(k2, ki, 11, O.arith_shift_right)
        ts(F("y"), k2, -1.0, O.mult, 4096.0, O.add)
        cp(ki, F("y"))
        ts(k2, ki, 4, O.arith_shift_right)
        cp(sig, k2)
        ts(k2, ki, 15, O.bitwise_and)
        cp(rnk, k2)
        vstep()
        if t == 0:
            cp(POS, sub(B2_, 256, 384))
            agents()
        build_xc(cl)
        gr, live, want0 = F("gr"), F("live"), F("want0")
        tt(gr, sub(B1, 32, 48), sig, O.subtract)
        ts(live, nc, 0.5, O.is_gt)
        ts(want0, gr, sub(lims, 1, 2), O.is_gt)
        tt(want0, want0, live, O.mult)
        ai0, ai1 = A("ai", 0, 256), A("ai", 256, 512)
        cp(ai0, A("acq"))
        ts(ai1, ai0, 15, O.bitwise_and)
        ts(ai0, ai0, 4, O.arith_shift_right)
        ts(A("ahl"), A("ai"), F("k128", 1), O.add, 1.0 / 2048, O.mult)
        scan(A("gt", 0, 2048), A("m0"), A("psA"), O.mult, O.max)
        lanes_of(A("gt", 0, 2048), ED2)
        vstep()
        if t:
            s_keys()
        for k in range(4):
            z0 = 1024 * (k % 2)
            c = (z0, z0 + 1024)
            cp(A("zb", z0, z0 + 1024, 16), A("xsb", 64 * k, 64 * k + 64))
            scan(A("xr", *c), A("mr", 0, 1024), A("zb", *c), O.mult, O.add)
            tt(A("df", *c), X(A("xc", 0, 2048), A("acq", 64 * k, 64 * k + 64)), A("xr", *c), O.subtract)
            act(A("df", *c), A("df", *c), AF.Square)
            for i in range(16):
                mm(A("psB", 64 * k, 64 * k + 64), bws(i), A("df", z0 + i, z0 + 1024, 16), i == 0, i == 15)
        if t:
            new_pos()
        sel(F("kb0"), 0)
        sel(F("kb1"), 1)
        cp(ki, F("kb0"))
        ts(ki, ki, 127, O.bitwise_and)
        cp(k2, F("kb1"))
        ts(k2, k2, 15, O.bitwise_and)
        bf = F("bf")
        ts(bf, ki, 16.0, O.mult)
        tt(bf, bf, k2, O.add)
        for h in (0, 1):
            tt(A("tg", 256 * h, 256 * h + 256), sub(B0, 0, 256), A("ahl", 256 * h, 256 * h + 256), O.add)
        vtr(A("tt"), A("tg"))
        scan(A("tg"), A("mrb"), A("tt"), O.max, O.min)
        r32 = S("si", "r32", 32)
        ts(r32, A("tg", 15, 512, 16), 2048.0, O.mult)
        ts(S("si", "rh"), sub(r32, 0, 16), 127, O.bitwise_and)
        ts(S("si", "rl"), sub(r32, 16, 32), 15, O.bitwise_and)
        ts(F("ah"), S("si", "rh"), 16.0, O.mult, -2048.0, O.add)
        tt(F("ah"), F("ah"), S("si", "rl"), O.add)
        ts(F("fit"), A("tg", 15, 256, 16), 4096.0, O.is_lt)
        tt(F("ah"), F("ah"), F("fit"), O.mult)
        ts(S("sh", "a16"), F("ah"), 2048.0, O.add)
        s2o(S("sh", "a16"), sub(B1, 48, 64), 16)
        has = F("has")
        ts(has, sub(B1, 48, 64), 2047.5, O.is_lt)
        tt(has, has, live, O.mult)
        ts(S("su", "aU"), sub(B1, 48, 64), 2047.0, O.min)
        cp(A("ag16"), X(A("at"), S("su", "aU")))
        gathO("ag16", 0, 256, setof("E"), sub(B1, 64, 80))
        gathO("ag16", 0, 256, setof("r8"), sub(B3, 480, 496))
        gathO("ag16", 0, 256, setof("n"), sub(B3, 496, 512))
        if t:
            u_scan()
            k_scan()
        DU, DD2 = S("su", "du"), S("su", "dd2", 32)
        for o in (DU, sub(DD2, 0, 32, 2), sub(DD2, 1, 32, 2)):
            ts(o, sub(B1, 64, 80), -1.0, O.add)
        dn, df_, d47 = F("dn"), F("d"), F("d47")
        cp(A("ud"), X(A("us"), DU))
        cp(dn, sub(B3, 496, 512))
        cp(df_, sub(B3, 480, 496))
        ts(d47, df_, -2047.0, O.add)
        tt(d47, d47, has, O.mult)
        ts(d47, d47, 2047.0, O.add)
        cp(S("sh", "d16"), d47)
        for w in range(16):
            mm(sub(B3, w, 256, 16), ors(w), S("sh", "d16"))
        tt(A("uv"), A("uc"), A("ud"), O.max)
        cp(A("drep"), sub(B3, 0, 256))
        for w in range(16):
            mm(sub(B1, 112, 128), bws(w), A("uv", w, 256, 16), w == 0, w == 15)
        for u in range(16):
            q0 = 256 * (u % 4)
            if u % 4 == u:
                if u:
                    ms(A("eq", q0, q0 + 16 * u), 0.0)
            else:
                ms(A("eq", q0 + 16 * (u - 4), q0 + 16 * u), 0.0)
            ts(A("eq", q0 + 16 * u, q0 + 256), A("drep", 16 * u, 256), sub(d47, u, u + 1), O.is_equal)
            tt(A("eq", q0 + 16 * u, q0 + 16 * u + 16), A("eq", q0 + 16 * u, q0 + 16 * u + 16), S("sb", "tri"), O.mult)
            mm(sub(B3, 256, 512), BB, A("eq", q0, q0 + 256), u == 0, u == 15)
        lanes_of(A("ks", 0, 2048), DD2)
        sel(F("key"), 0, F("mE4", 1), F("mO4", 1))
        cp(ki, F("key"))
        ts(k2, ki, 11, O.arith_shift_right)
        ts(F("y"), k2, -1.0, O.mult, 4096.0, O.add)
        cp(ki, F("y"))
        ts(k2, ki, 4, O.arith_shift_right)
        cp(F("sigd"), k2)
        mer, tmp = F("mer"), F("tmp")
        tt(tmp, F("sigd"), sig, O.min)
        tt(tmp, sub(B1, 112, 128), tmp, O.subtract)
        ts(mer, tmp, limz, O.is_le)
        tt(tmp, nc, dn, O.add)
        ts(tmp, tmp, 16.5, O.is_lt)
        tt(mer, mer, tmp, O.mult)
        tt(mer, mer, has, O.mult)
        vtr(A("ctr"), sub(B3, 256, 512))
        cp(S("sh", "ct"), A("ctr", 0, 256, 16))
        s2o(S("sh", "ct"), sub(B1, 128, 144), 16)
        ts(tmp, sub(B1, 128, 144), 0.5, O.is_lt)
        tt(mer, mer, tmp, O.mult)
        want, spl, wk = F("want"), F("spl"), F("wk")
        ts(tmp, mer, -1.0, O.mult, 1.0, O.add)
        tt(want, want0, tmp, O.mult)
        cp(S("sb", "wb"), want)
        prefix(S("sb", "wb"), 16, wk, "pw", sub(B1, 144, 176))
        ts(tmp, wk, F("ecnt", 1), O.is_lt)
        tt(spl, want, tmp, O.mult)
        cp(S("su", "kU"), wk)
        cp(A("eg16"), X(A("el"), S("su", "kU")))
        choose(bf, spl, bf, sf)
        cp(S("su", "bU"), bf)
        cp(A("xbb"), X(A("xa", 0, 2048), S("su", "bU")))
        cp(A("xb", *lanes), A("xbb"))
        idle, visit, vk = F("idle"), F("visit"), F("vk")
        tt(tmp, mer, spl, O.add)
        tt(idle, live, tmp, O.subtract)
        cp(S("sb", "ib"), idle)
        prefix(S("sb", "ib"), 16, vk, "pv", sub(B1, 208, 240))
        x1, x2 = S("sh", "x1", 48), S("sh", "x2")
        tt(tmp, mer, dn, O.mult)
        tt(sub(x1, 0, 16), nc, tmp, O.add)
        cp(sub(x1, 16, 32), nc)
        cp(sub(x1, 32, 48), df_)
        for w in range(16):
            mm(A("psA", w, 512, 16), ors(w), sub(x1, 0, 32))
            mm(A("psA", 512 + w, 768, 16), ors(w), sub(x1, 32, 48))
        act(A("x16", 0, 768), A("psA", 0, 768), AF.Copy)
        xr_, xn_, xd_, xl_ = [A("x16", 256 * k, 256 * k + 256) for k in range(4)]
        ckl = A("ck16", cl, 1024, 4)
        p0, p1, p2 = sub(B0, 0, 256), sub(B0, 256, 512), sub(B3, 0, 256)
        mms(p0, [(M237, xr_), (I16, ckl)])
        gathO("eg16", 0, 256, setof("r8"), sub(B1, 176, 192))
        if t:
            gathO("g16", 0, 2048, s0s, sub(B2_, 0, 128))
        gathO("rk", 0, 2048, s0s, sub(B2_, 384, 512))
        for k in range(4):
            c = (512 * k, 512 * k + 512)
            tt(A("df", *c), X(A("xb"), chunks(CQ, k, 4)), A("xs", *c), O.subtract)
            act(A("df", *c), A("df", *c), AF.Square)
            mms(A("psA", *c), [(BBN, A("sqs", *c)), (BB, A("df", *c))])
        tl = F("tl")
        ts(tl, lane, 1280.0, O.add)
        choose(tmp, mer, df_, tl)
        cp(S("su", "dL"), tmp)
        cp(A("sz", cl, 1024, 4), p0)
        cp(X(A("sz"), S("su", "dL")), A("zd"))
        scan(A("bt", 0, 1024), A("d0"), A("sz", 0, 1024), O.mult, O.add)
        cp(A("bl16"), A("bt", cl, 1024, 4))
        choose(tmp, spl, sub(B1, 176, 192), tl)
        cp(S("su", "eL"), tmp)
        ts(visit, vk, 95.5, O.is_lt)
        tt(visit, visit, idle, O.mult)
        ts(tl, lane, 96.0, O.add)
        choose(tmp, visit, vk, tl)
        cp(S("su", "vL"), tmp)
        cp(X(A("vs"), S("su", "vL")), A("xsb"))
        q = T.cores[(rank + 1 + t % 7) % 8]
        h = T.cores[(rank - 1 - t % 7) % 8]
        send(q, "in%d" % t, A("vs", 0, 96), "ra%d" % t, "la%d" % t)
        ts(tl, lane, 2048.0, O.add)
        choose(tmp, visit, sf, tl)
        cp(S("su", "vA"), tmp)
        cp(A("res", 96, 352), A("xsb"))
        if t:
            cp(POS, sub(B2_, 0, 128))
        for k in range(4):
            c = (512 * k, 512 * k + 512)
            ts(A("g16", *c), A("psA", *c), 0.0, O.is_lt)
        cp(A("xb", *lanes), A("xsb"))
        scan(A("rl"), A("m0"), A("g16"), O.mult, O.add)
        gathO("g16", 0, 2048, s0s, sub(B2_, 0, 128))
        lanes_of(A("rl"), ED2)
        nl = F("nl")
        sel(nl, 0)
        tt(nl, nl, spl, O.mult)
        cv, lv, cql, rp = F("cv", 128), F("lv", 128), F("cql", 128), F("rp", 128)
        rkO, rlO = F("rkO", 128), F("rlO", 128)
        cp(rkO, sub(B2_, 384, 512))
        cp(x2, nl)
        for w in range(16):
            mm(sub(p2, w, 256, 16), ors(w), x2)
        cp(xl_, p2)
        mms(p0, [(I16, A("bl16")), (M7N, xl_)])
        mms(p1, [(I16, A("bl16")), (M5, xn_), (M1N, xd_), (M81, ckl), (M7N, xl_)])
        mms(p2, [(I23, A("bl16")), (M56, xn_), (M567, xl_), (IX, A("eg16")), (M81N, ckl)])
        gathO("rl", 0, 2048, bws, sub(B1, 256, 384))
        cp(lv, sub(B2_, 0, 128))
        ts(cv, CQF, -0.75, O.mult, 1024.0 - cl / 4.0, O.add)
        tt(cv, cv, lv, O.mult)
        tt(cql, cv, CQF, O.add)
        cp(S("su", "cqL", 128), cql)
        gathO("bl16", 0, 256, setof("np"), sub(B2_, 192, 208))
        cp(A("bt", cl, 1024, 4), p0)
        cp(A("bt", 1024, 1280), p2)
        cp(A("lft"), p2)
        cp(A("dvt"), p1)
        cp(X(A("bt"), S("su", "eL")), A("lft"))
        if t < 3:
            cp(A("lt16"), A("bt", cl + 1, 1024, 4))
        else:
            cp(A("bt16"), A("bt", 0, 1024))
        cp(X(A("bt"), S("su", "dL")), A("dvt"))
        for k in range(4):
            act(A("gt", 512 * k, 512 * k + 512), X(A("bt", 0, 1280), chunks(S("su", "cqL", 128), k, 4)), AF.Copy)
        cp(A("g16"), X(A("bt", 0, 1280), S("su", "cqL", 128)))
        mms(p0, [(M237, xr_), (M237N, xl_), (I16, ckl)])
        mms(p1, [(M237, xl_), (I16, A("eg16"))])
        gathO("g16", 0, 2048, setof("np"), sub(B3, 256, 384))
        cp(A("sz", cl, 1024, 4), p0)
        cp(A("sze"), p1)
        cp(X(A("sz"), S("su", "eL")), A("sze"))
        agents()
        ts(rlO, sub(B1, 256, 384), 0.0625, O.mult)
        tt(rp, rkO, rlO, O.subtract)
        tt(rlO, rlO, rp, O.subtract)
        ts(rlO, rlO, -1.0, O.add)
        tt(rlO, rlO, lv, O.mult)
        tt(rp, rp, rlO, O.add)
        stc = F("stc")
        cp(stc, sub(B2_, 192, 208))
        tt(stc, stc, rnk, O.add)
        ts(tl, lane, 2048.0, O.add)
        choose(tmp, visit, stc, tl)
        cp(S("su", "vP"), tmp)
        tt(rp, rp, sub(B3, 256, 384), O.add)
        cp(S("su", "npL", 128), rp)
        if t < 3:
            cp(S("sh", "rp16", 128), rp)
            for w in range(16):
                for k in range(4):
                    mm(A("psA", 512 * k + w, 512 * k + 512, 16), ors(w), chunks(S("sh", "rp16", 128), k, 4))
            act(A("ks", 2080, 4128), A("psA"), AF.Copy)
        tt(X(A(R[1]), S("su", "npL", 128)), A("gt", 0, 2048), A(R[0]), O.add)
        R = R[::-1]
        gens[:] = [visits(t, q, h)]
        vstep()
        if t < 3:
            empties()
        order_tables(R[0], t == 3)
        if t < 3:
            mt = S("sb", "mt")
            cp(mt, mer)
            mm(sub(B1, 240, 256), o128, mt)
            emit("v", lambda: g.vector.tensor_reduce(ap(F("zz", 1)), ap(sub(B1, 240, 256)), AX.X, O.add), [F("zz", 1)], [sub(B1, 240, 256)])
            zi = S("si", "zi", 1)
            cp(zi, F("zz", 1))
            ts(zi, zi, 15, O.bitwise_and)
            tt(limz, sub(lims, 0, 1), zi, O.add)
    for k in range(4):
        mm(A("psA", 512 * k, 512 * k + 512), RPP, A("r16", 16 + 512 * k, 528 + 512 * k))
        act(A("ks", 512 * k, 512 * k + 512), A("psA", 512 * k, 512 * k + 512), AF.Copy)
    ms(A("ks", 2048, 2080), 2048.0)
    fin.append(dmas("y", [(A("gt", 0, 2048), A("ks"), T["gt"][k::16, 0:2048], T["ks"][k::16, k:k + 2048]) for k in range(16)]))
    gathO("bt16", 0, 1024, setof("st"), sub(B2_, 0, 64))
    ts(S("su", "l64", 64), sub(B2_, 0, 64), 2047.0, O.min)
    vstep()
    for k in range(2):
        mm(A("psA", 512 * k, 512 * k + 512), NRP, A("bt16", 512 * k, 512 * k + 512))
    ye, yb = A("el", 0, 1024), A("bt", 0, 1024)
    ts(yb, A("psA", 0, 1024), kcol, O.is_gt)
    vstep()
    vstep()
    cp(ye, X(A("gt", 0, 2048), S("su", "l64", 64)))
    ts(ye, ye, -2048.0, O.add)
    tt(ye, ye, yb, O.mult)
    ts(ye, ye, 2048.0, O.add)
    fin.append(dmas("y", [(None, ye, T.ym[:, 0:1024], T["el"][:, 0:1024])]))
    vstep()
    fin.append(dmas("y", [(None, A("xa", 0, 2048), T.yx[:, 0:2048], T["xa"][:, 0:2048])]))
    for who, v in fin + [(e, cnt[e]) for e in ("v", "s", "t", "g")]:
        g.wait_ge(T.sem[SEM[who]], v)
